import numpy as np
import ml_dtypes


def mxq(x, axis, fmt="e4m3"):
    dtype, down = {"e4m3": (ml_dtypes.float8_e4m3fn, 7), "e5m2": (ml_dtypes.float8_e5m2, 14)}[fmt]
    v = np.moveaxis(np.asarray(x, np.float32).astype(ml_dtypes.bfloat16).astype(np.float64), axis, -1)
    blocks = v.reshape(v.shape[:-1] + (-1, 32))
    amax = np.abs(blocks).max(-1, keepdims=True)
    byte = np.maximum(np.where(amax > 0, np.frexp(amax)[1] - 1 + 127, 0) - down, 1)
    scale = np.exp2(byte - 127.0)
    codes = (blocks / scale).astype(np.float32).astype(dtype).astype(np.float64)
    return np.moveaxis((codes * scale).reshape(v.shape), -1, axis)


WIDE = False


def mx_kscale(k):
    if not WIDE:
        return np.ones(k)
    levels = np.array([30, -30])
    if k % 512:
        return np.exp2(np.random.permutation(np.resize(levels, k // 32))).repeat(32)
    a = np.empty((k // 512, 16))
    for p in range(k // 512):
        a[p, :8] = np.random.permutation(np.resize(levels, 8))
        for g in range(8):
            far = levels[np.abs(levels - a[p, g]) >= 10]
            a[p, g + 8] = far[np.random.randint(len(far))]
    return np.exp2(a.ravel()).repeat(32)


BF16 = ml_dtypes.bfloat16


def bf(x):
    return np.asarray(x, np.float32).astype(BF16)


def f64(x):
    return np.asarray(x).astype(np.float64)

E4M3FN = np.array([(-1.0 if i & 128 else 1.0) * ((1.0 + (i & 7) / 8.0) * 2.0 ** (((i >> 3) & 15) - 7) if i & 120 else (i & 7) * 2.0 ** -9) for i in range(256)])


def e4m3fn_bytes(y):
    return np.clip(np.asarray(y, np.float64), -448.0, 448.0).astype(np.float32).astype(ml_dtypes.float8_e4m3fn).view(np.uint8)


def e4m3fn_values(b):
    return E4M3FN[b]

def planes(Y):
    n, m = Y.shape
    b = f64(bf(Y)).reshape(n // 32, 32, m)
    amax = np.abs(b).max(1)
    byte = np.clip(np.where(amax > 0, np.frexp(amax)[1] - 1 + 127 - 7, 1), 1, 254)
    codes = (b * np.exp2(127.0 - byte)[:, None, :]).reshape(n, m).astype(np.float32).astype(ml_dtypes.float8_e4m3fn).view(np.uint8)
    words = codes.reshape(n // 512, 128, 4, m).transpose(0, 1, 3, 2)
    return np.ascontiguousarray(words), np.ascontiguousarray(byte.astype(np.uint8).reshape(n // 512, 16, m))


T, N, K, B = 3072, 1024, 1024, 32

MU = 0.9
RATE = 0.4


def setup_inputs():
    s = mx_kscale(T)
    c = np.exp(0.8 * np.random.randn(1, K))
    tail = np.exp(np.random.randn(N, T))
    Et = np.random.randn(N, T) * tail / (np.e * np.sqrt(T)) * s[None, :]
    Et_scale = (np.abs(Et).reshape(N, T // B, B).max(axis=2) / 448.0).astype(np.float32)
    Et_bytes = e4m3fn_bytes(Et / np.repeat(f64(Et_scale), B, axis=1))
    A = np.random.randn(T, K) * c / s[:, None]
    Mom = 0.8 * np.random.randn(N, K) * c
    W = np.random.randn(N, K) * c
    rate = RATE * np.exp(0.3 * np.random.randn(N, 1))
    return {"Et_bytes": Et_bytes, "Et_scale": Et_scale, "A": bf(A),
            "Mom": bf(Mom), "W": bf(W), "rate": bf(rate)}


def reference(Et_bytes, Et_scale, A, Mom, W, rate):
    Et = e4m3fn_values(Et_bytes) * np.repeat(f64(Et_scale), B, axis=1)
    G = mxq(Et, 1, "e5m2") @ mxq(f64(A), 0, "e4m3")
    mom_new = MU * f64(Mom) + G
    w_new = W_step = f64(W) - f64(rate) * mom_new
    y = np.stack([mom_new, w_new], axis=0)
    Y = y.reshape(-1, K).T
    words, scales = planes(Y)
    return y, words, scales

@@ -1,0 +1,418 @@
+from contextlib import ExitStack
+
+import concourse.mybir as mybir
+from concourse.masks import make_identity
+
+T, N, K, B = 3072, 1024, 1024, 32
+MU = 0.9
+FLOPS = 2 * T * N * K
+
+F32 = mybir.dt.float32
+BF16 = mybir.dt.bfloat16
+I32 = mybir.dt.int32
+U32 = mybir.dt.uint32
+U8 = mybir.dt.uint8
+FP8 = mybir.dt.float8_e4m3fn
+E4M3X4 = mybir.dt.float8_e4m3fn_x4
+E5M2X4 = mybir.dt.float8_e5m2_x4
+MULT = mybir.AluOpType.mult
+ADD = mybir.AluOpType.add
+COPY = mybir.ActivationFunctionType.Copy
+
+P = 128
+PACK = 4
+PASS = P * PACK
+PASSES = T // PASS
+HALF = 512
+HALVES = K // HALF
+TILES = N // P
+STEP = 2 * PASS
+STEPS_PER_TILE = T // STEP
+STEPS = TILES * STEPS_PER_TILE
+CHUNKS = PASSES * HALVES
+UNITS = TILES * HALVES
+
+ACC_BANKS = 4
+A_SLOTS = 12
+A_LAG = 4
+FIRST_UNIT_SLOT = 12
+MM_CAP = 5
+MM_START = 5
+CAP_FROM = -20
+T_LAG = 2
+Y_LAG = 3
+COPY_PERIOD = 2
+VECTOR_COPY_FROM = 10
+SCALAR_CAST_FROM = 12
+
+
+def tile_vision_momentum_sgd_step_b13_kernel(
+    tc, Et_bytes, Et_scale, A, Mom, W, rate, out_0, out_1, out_2
+):
+    nc = tc.nc
+    words_out = out_1.rearrange("g p m t -> g p (m t)").bitcast(I32)
+    scales_out = out_2.bitcast(I32)
+
+    with ExitStack() as ctx:
+        keep = ctx.enter_context(tc.tile_pool(name="keep", bufs=1))
+        flow = ctx.enter_context(tc.tile_pool(name="flow", bufs=3))
+        psum = ctx.enter_context(tc.psum_pool(name="psum", bufs=2))
+        ctx.enter_context(tc.manual_schedule())
+
+        ident = keep.tile([P, P], F32)
+        make_identity(nc, ident[:])
+        rate_rows = keep.tile([P, P], BF16)
+        nc.gpsimd.memset(rate_rows[:], 0.0)
+        ident_bf = keep.tile([P, P], BF16)
+        make_identity(nc, ident_bf[:])
+        neg_rate = keep.tile([P, TILES], F32)
+
+        et_scale = {}
+        et_bytes = {}
+        a_raw = {}
+        mom_old = {}
+        w_old = {}
+
+        def load_scales(first, count):
+            t = keep.tile([P, count * (T // B)], F32, name="et_scale%d" % first)
+            nc.sync.dma_start(
+                out=t[:].rearrange("p (i b) -> p i b", i=count),
+                in_=Et_scale[first * P : (first + count) * P, :].rearrange("(i p) b -> p i b", p=P),
+            )
+            for i in range(count):
+                et_scale[first + i] = t[:, i * (T // B) : (i + 1) * (T // B)]
+
+        def load_et(i, b0, b1, name, bufs):
+            t = flow.tile([P, (b1 - b0) * STEP], U8, name=name, bufs=bufs)
+            nc.sync.dma_start(out=t[:], in_=Et_bytes[i * P : (i + 1) * P, b0 * STEP : b1 * STEP])
+            for b in range(b0, b1):
+                et_bytes[STEPS_PER_TILE * i + b] = t[:, (b - b0) * STEP : (b - b0 + 1) * STEP]
+
+        def load_a(c):
+            g, h = divmod(c, HALVES)
+            t = flow.tile([P, PACK, HALF], BF16, name="a_raw", bufs=8)
+            rows = A[g * PASS : (g + 1) * PASS, h * HALF : (h + 1) * HALF]
+            nc.sync.dma_start(out=t[:], in_=rows.rearrange("(p j) k -> p j k", j=PACK))
+            a_raw[c] = t
+
+        def load_state(pair):
+            for src, dst, name in ((Mom, mom_old, "mom_old%d"), (W, w_old, "w_old%d")):
+                t = keep.tile([P, 2, K], BF16, name=name % pair)
+                rows = src[2 * pair * P : 2 * (pair + 1) * P, :]
+                nc.sync.dma_start(out=t[:], in_=rows.rearrange("(i p) k -> p i k", p=P))
+                for i in range(2):
+                    dst[2 * pair + i] = t[:, i, :]
+
+        def load_rate():
+            nc.sync.dma_start(out=rate_rows[0:TILES, :], in_=rate.rearrange("(i p) o -> i (p o)", p=P))
+
+        def make_neg_rate():
+            bank = psum.tile([P, P], BF16, name="et_bank")
+            nc.tensor.transpose(bank[:], rate_rows[:], ident_bf[:])
+            nc.scalar.activation(out=neg_rate[:], in_=bank[:, 0:TILES], func=COPY, scale=-1.0)
+
+        a_grouped = {}
+        a_codes = {}
+        a_scales = {}
+
+        def interleave_a(c):
+            t = flow.tile([P, HALF * PACK], BF16, name="a_grouped", bufs=2, align_bytes=64)
+            nc.vector.tensor_copy(
+                out=t[:].rearrange("p (c i j) -> p c j i", i=4, j=PACK),
+                in_=a_raw[c][:].rearrange("p j (c i) -> p c j i", i=4),
+            )
+            a_grouped[c] = t
+
+        def quantize_a(c):
+            codes = keep.tile([P, HALF], U32, name="a_codes%d" % c, align_bytes=64)
+            scales = keep.tile([P, HALF], U8, name="a_scales%d" % c, align_bytes=64)
+            nc.vector.quantize_mx(out=codes[:].bitcast(E4M3X4), scales=scales[:], in_=a_grouped[c][:])
+            a_codes[c] = codes
+            a_scales[c] = scales
+
+        et_wide = {}
+        et_bank = {}
+        et_grouped = {}
+        et_codes = {}
+        et_scales = {}
+
+        def widen(s):
+            i, b = divmod(s, STEPS_PER_TILE)
+            t = flow.tile([P, STEP], BF16, name="et_wide")
+            for q in range(STEP // B):
+                block = b * (STEP // B) + q
+                nc.scalar.activation(
+                    out=t[:, q * B : (q + 1) * B],
+                    in_=et_bytes[s][:, q * B : (q + 1) * B].bitcast(FP8),
+                    func=COPY,
+                    scale=et_scale[i][:, block : block + 1],
+                )
+            et_wide[s] = t
+
+        def turn_et(s):
+            bank = psum.tile([P, 4 * P], F32, name="et_bank")
+            pairs = et_wide[s][:].bitcast(F32)
+            for g in range(2):
+                for u in range(2):
+                    nc.tensor.transpose(
+                        bank[:, (2 * g + u) * P : (2 * g + u + 1) * P],
+                        pairs[:, 2 * P * g + u : 2 * P * (g + 1) : 2],
+                        ident[:],
+                    )
+            et_bank[s] = bank
+
+        def copy_bank(engine_copy, bank, name):
+            t = flow.tile([P, 2 * PASS], BF16, name=name, bufs=5, align_bytes=64)
+            engine_copy(
+                out=t[:].bitcast(F32).rearrange("p (g r u) -> p g r u", g=2, u=2),
+                in_=bank[:].rearrange("p (g u r) -> p g r u", g=2, u=2),
+            )
+            return t
+
+        def copy_et(s):
+            engine_copy = nc.vector.tensor_copy if STEPS - 1 > s >= VECTOR_COPY_FROM and (s - VECTOR_COPY_FROM + 1) % COPY_PERIOD else nc.scalar.copy
+            et_grouped[s] = copy_bank(engine_copy, et_bank[s], "et_grouped")
+
+        def quantize_et(s):
+            codes = flow.tile([P, 2 * P], U32, name="et_codes", bufs=12, align_bytes=64)
+            scales = flow.tile([P, 2 * P], U8, name="et_scales", bufs=12, align_bytes=64)
+            nc.vector.quantize_mx(out=codes[:].bitcast(E5M2X4), scales=scales[:], in_=et_grouped[s][:])
+            et_codes[s] = codes
+            et_scales[s] = scales
+
+        def acc_bank(j):
+            return j if j < 6 else (0, 1, 4, 5)[(j - 6) % 4]
+
+        def bank_before(j):
+            return max(x for x in range(j) if acc_bank(x) == acc_bank(j))
+
+        acc = {}
+        done = set()
+
+        def multiply(j, g):
+            i, h = divmod(j, HALVES)
+            if g == 0:
+                acc[j] = psum.tile([P, HALF], F32, name="acc", tag="bank%d" % acc_bank(j), bufs=1)
+            s = STEPS_PER_TILE * i + g // 2
+            cols = slice((g % 2) * P, (g % 2 + 1) * P)
+            c = HALVES * g + h
+            nc.tensor.matmul_mx(
+                out=acc[j][:],
+                lhsT=et_codes[s][:, cols].bitcast(E5M2X4),
+                lhsT_scale=et_scales[s][:, cols],
+                rhs=a_codes[c][:].bitcast(E4M3X4),
+                rhs_scale=a_scales[c][:],
+                start=(g == 0),
+                stop=(g == PASSES - 1),
+            )
+
+        y = {}
+        y_sorted = {}
+        y_bank = {}
+        y_grouped = {}
+        y_codes = {}
+        y_scales = keep.tile([P, HALVES * 2 * N], U8, align_bytes=64)
+
+        def new_momentum(j):
+            i, h = divmod(j, HALVES)
+            assert (j, PASSES - 1) in done
+            t = flow.tile([P, 2 * HALF], F32, name="y", bufs=5)
+            nc.vector.scalar_tensor_tensor(
+                out=t[:, 0:HALF], in0=mom_old[i][:, h * HALF : (h + 1) * HALF], scalar=MU,
+                in1=acc[j][:], op0=MULT, op1=ADD,
+            )
+            y[j] = t
+
+        def new_weights(j):
+            i, h = divmod(j, HALVES)
+            nc.vector.scalar_tensor_tensor(
+                out=y[j][:, HALF : 2 * HALF], in0=y[j][:, 0:HALF], scalar=neg_rate[:, i : i + 1],
+                in1=w_old[i][:, h * HALF : (h + 1) * HALF], op0=MULT, op1=ADD,
+            )
+            nc.sync.dma_start(
+                out=out_0[:, i * P : (i + 1) * P, h * HALF : (h + 1) * HALF].rearrange("s p k -> p s k"),
+                in_=y[j][:].rearrange("p (s k) -> p s k", s=2),
+            )
+
+        def round_y(j, engine_copy):
+            t = flow.tile([P, 2 * HALF], BF16, name="y_sorted", bufs=4)
+            engine_copy(
+                out=t[:].rearrange("p (u q e) -> p u q e", u=2, e=2),
+                in_=y[j][:].rearrange("p (q u e) -> p u q e", u=2, e=2),
+            )
+            y_sorted[j] = t
+
+        def turn_y(j):
+            bank = psum.tile([P, 4 * P], F32, name="y_bank", tag="bank%d" % (2 + j % 2), bufs=1)
+            pairs = y_sorted[j][:].bitcast(F32)
+            for s in range(2):
+                for u in range(2):
+                    nc.tensor.transpose(
+                        bank[:, (2 * s + u) * P : (2 * s + u + 1) * P],
+                        pairs[:, (2 * u + s) * P : (2 * u + s + 1) * P],
+                        ident[:],
+                    )
+            y_bank[j] = bank
+
+        def copy_y(j):
+            y_grouped[j] = copy_bank(nc.scalar.copy, y_bank[j], "y_grouped")
+
+        def quantize_y(j):
+            i, h = divmod(j, HALVES)
+            pair, second = divmod(i, 2)
+            if second == 0:
+                y_codes[pair, h] = flow.tile([P, 4 * P], U32, name="y_codes", bufs=6, align_bytes=64)
+            codes = y_codes[pair, h]
+            for s in range(2):
+                nc.vector.quantize_mx(
+                    out=codes[:, (2 * s + second) * P : (2 * s + second + 1) * P].bitcast(E4M3X4),
+                    scales=y_scales[:, (2 * h + s) * N + i * P : (2 * h + s) * N + (i + 1) * P],
+                    in_=y_grouped[j][:, s * PASS : (s + 1) * PASS],
+                )
+            if second == 1:
+                nc.sync.dma_start(
+                    out=words_out[h].rearrange("p (s n) -> p s n", s=2)[:, :, 2 * pair * P : 2 * (pair + 1) * P],
+                    in_=codes[:].bitcast(I32).rearrange("p (s n) -> p s n", s=2),
+                )
+            if j == UNITS - 1:
+                for q in range(4):
+                    (nc.sync, nc.scalar)[q % 2].dma_start(
+                        out=scales_out[:, 4 * q : 4 * q + 4, :].rearrange("h r m -> r h m"),
+                        in_=y_scales[32 * q : 32 * q + 4, :].bitcast(I32).rearrange("r (h m) -> r h m", h=HALVES),
+                    )
+
+        load_scales(0, 1)
+        load_et(0, 0, 1, "et_first", 1)
+        load_a(0)
+        load_et(0, 1, STEPS_PER_TILE, "et_second", 1)
+        load_a(1)
+        load_scales(1, TILES - 1)
+        load_a(2)
+        load_a(3)
+        load_et(1, 0, STEPS_PER_TILE, "et_bytes", 4)
+        load_a(4)
+        load_a(5)
+        load_rate()
+        load_et(2, 0, STEPS_PER_TILE, "et_bytes", 4)
+        load_a(6)
+        load_a(7)
+
+        def late_loads(slot):
+            if slot == 2:
+                load_a(8)
+                load_state(0)
+            if slot == 3:
+                load_a(9)
+                load_et(3, 0, STEPS_PER_TILE, "et_bytes", 4)
+            if slot == 4:
+                load_a(10)
+                load_et(4, 0, STEPS_PER_TILE, "et_bytes", 4)
+            if slot == 5:
+                load_a(11)
+                load_state(1)
+            if slot == 6:
+                load_et(5, 0, STEPS_PER_TILE, "et_bytes", 4)
+                load_state(2)
+                load_state(3)
+            if slot == 9:
+                load_et(6, 0, STEPS_PER_TILE, "et_bytes", 4)
+            if slot == 12:
+                load_et(7, 0, STEPS_PER_TILE, "et_bytes", 4)
+
+        def within(index, count):
+            return 0 <= index < count
+
+        chunk_slot = [c * A_SLOTS // CHUNKS for c in range(CHUNKS)]
+
+        def ready(j, g, slot):
+            i, h = divmod(j, HALVES)
+            et_done = STEPS_PER_TILE * i + g // 2 + 2 <= slot
+            a_done = chunk_slot[HALVES * g + h] + (2 if g < A_LAG else 1) <= slot
+            bank_free = j < 6 or FIRST_UNIT_SLOT + bank_before(j) <= slot
+            return et_done and a_done and bank_free and slot >= MM_START
+
+        interleaved = []
+        for slot in range(STEPS):
+            j = slot - FIRST_UNIT_SLOT
+            late_loads(slot)
+            if slot == 8:
+                make_neg_rate()
+            if within(slot - 1, STEPS):
+                turn_et(slot - 1)
+            if within(j, UNITS):
+                new_momentum(j)
+            if within(j - 1, UNITS):
+                round_y(j - 1, nc.vector.tensor_copy)
+            if within(j - T_LAG, UNITS):
+                turn_y(j - T_LAG)
+            if within(slot, STEPS):
+                widen(slot)
+            chunks = [c for c in range(CHUNKS) if chunk_slot[c] == slot]
+            for c in chunks:
+                interleave_a(c)
+                if interleaved:
+                    quantize_a(interleaved.pop())
+                interleaved.append(c)
+            if not chunks and interleaved:
+                quantize_a(interleaved.pop())
+            if within(j - Y_LAG, UNITS):
+                quantize_y(j - Y_LAG)
+            if within(j, UNITS):
+                new_weights(j)
+            if within(slot - 2, STEPS):
+                quantize_et(slot - 2)
+            if within(slot - 1, STEPS):
+                copy_et(slot - 1)
+            if within(j - T_LAG, UNITS):
+                copy_y(j - T_LAG)
+            waiting = [(unit, g) for unit in range(UNITS) for g in range(PASSES) if (unit, g) not in done]
+            for unit, g in [x for x in waiting if ready(x[0], x[1], slot)][: MM_CAP if CAP_FROM <= j and slot < STEPS else None]:
+                multiply(unit, g)
+                done.add((unit, g))
+
+        def multiply_rest(passes):
+            for unit in range(UNITS):
+                for g in range(passes):
+                    if (unit, g) not in done:
+                        multiply(unit, g)
+                        done.add((unit, g))
+
+        assert FIRST_UNIT_SLOT == 12
+        turn_et(23)
+        turn_y(10)
+        quantize_et(22)
+        multiply_rest(4)
+        round_y(11, nc.scalar.copy)
+        copy_et(23)
+        copy_y(10)
+        new_momentum(12)
+        quantize_y(9)
+        new_weights(12)
+        quantize_et(23)
+        multiply_rest(6)
+        turn_y(11)
+        round_y(12, nc.scalar.copy)
+        copy_y(11)
+        new_momentum(13)
+        quantize_y(10)
+        new_weights(13)
+        turn_y(12)
+        round_y(13, nc.scalar.copy)
+        copy_y(12)
+        new_momentum(14)
+        new_momentum(15)
+        new_weights(14)
+        new_weights(15)
+        turn_y(13)
+        copy_y(13)
+        round_y(14, nc.vector.tensor_copy)
+        round_y(15, nc.vector.tensor_copy)
+        turn_y(14)
+        copy_y(14)
+        turn_y(15)
+        copy_y(15)
+        quantize_y(11)
+        quantize_y(12)
+        quantize_y(13)
+        quantize_y(14)
+        quantize_y(15)

@@ -38,6 +38,11 @@ A_LAG = 4
 FIRST_UNIT_SLOT = 12
 MM_CAP = 5
 MM_START = 5
+A_PERIOD = 2
+ET_LAG = 2
+BANK_LAG = 0
+B_PERIOD = 4
+CAP_LAST = 0
 CAP_FROM = -20
 T_LAG = 2
 Y_LAG = 3
@@ -82,11 +87,11 @@ def tile_vision_momentum_sgd_step_b13_kernel(
             for i in range(count):
                 et_scale[first + i] = t[:, i * (T // B) : (i + 1) * (T // B)]
 
-        def load_et(i, b0, b1, name, bufs):
-            t = flow.tile([P, (b1 - b0) * STEP], U8, name=name, bufs=bufs)
-            nc.sync.dma_start(out=t[:], in_=Et_bytes[i * P : (i + 1) * P, b0 * STEP : b1 * STEP])
-            for b in range(b0, b1):
-                et_bytes[STEPS_PER_TILE * i + b] = t[:, (b - b0) * STEP : (b - b0 + 1) * STEP]
+        def load_et(i, g0, g1, name, bufs):
+            t = flow.tile([P, (g1 - g0) * PASS], U8, name=name, bufs=bufs)
+            nc.sync.dma_start(out=t[:], in_=Et_bytes[i * P : (i + 1) * P, g0 * PASS : g1 * PASS])
+            for g in range(g0, g1):
+                et_bytes[i, g] = t[:, (g - g0) * PASS : (g - g0 + 1) * PASS]
 
         def load_a(c):
             g, h = divmod(c, HALVES)
@@ -136,49 +141,58 @@ def tile_vision_momentum_sgd_step_b13_kernel(
         et_codes = {}
         et_scales = {}
 
+        steps = [(i, range(g, g + 2)) for i in range(TILES) for g in range(0, PASSES, 2)]
+        steps = steps[:-1] + [(TILES - 1, range(g, g + 1)) for g in (PASSES - 2, PASSES - 1)]
+        step_of = {(i, g): s for s, (i, passes) in enumerate(steps) for g in passes}
+
         def widen(s):
-            i, b = divmod(s, STEPS_PER_TILE)
-            t = flow.tile([P, STEP], BF16, name="et_wide")
-            for q in range(STEP // B):
-                block = b * (STEP // B) + q
-                nc.scalar.activation(
-                    out=t[:, q * B : (q + 1) * B],
-                    in_=et_bytes[s][:, q * B : (q + 1) * B].bitcast(FP8),
-                    func=COPY,
-                    scale=et_scale[i][:, block : block + 1],
-                )
+            i, passes = steps[s]
+            t = flow.tile([P, len(passes) * PASS], BF16, name="et_wide")
+            for n, g in enumerate(passes):
+                for q in range(PASS // B):
+                    block = g * (PASS // B) + q
+                    nc.scalar.activation(
+                        out=t[:, n * PASS + q * B : n * PASS + (q + 1) * B],
+                        in_=et_bytes[i, g][:, q * B : (q + 1) * B].bitcast(FP8),
+                        func=COPY,
+                        scale=et_scale[i][:, block : block + 1],
+                    )
             et_wide[s] = t
 
         def turn_et(s):
-            bank = psum.tile([P, 4 * P], F32, name="et_bank")
+            count = len(steps[s][1])
+            bank = psum.tile([P, count * 2 * P], F32, name="et_bank")
             pairs = et_wide[s][:].bitcast(F32)
-            for g in range(2):
+            for n in range(count):
                 for u in range(2):
                     nc.tensor.transpose(
-                        bank[:, (2 * g + u) * P : (2 * g + u + 1) * P],
-                        pairs[:, 2 * P * g + u : 2 * P * (g + 1) : 2],
+                        bank[:, (2 * n + u) * P : (2 * n + u + 1) * P],
+                        pairs[:, 2 * P * n + u : 2 * P * (n + 1) : 2],
                         ident[:],
                     )
             et_bank[s] = bank
 
         def copy_bank(engine_copy, bank, name):
-            t = flow.tile([P, 2 * PASS], BF16, name=name, bufs=5, align_bytes=64)
+            t = flow.tile([P, 2 * bank.shape[1]], BF16, name=name, bufs=7, align_bytes=64)
             engine_copy(
-                out=t[:].bitcast(F32).rearrange("p (g r u) -> p g r u", g=2, u=2),
-                in_=bank[:].rearrange("p (g u r) -> p g r u", g=2, u=2),
+                out=t[:].bitcast(F32).rearrange("p (n r u) -> p n r u", r=P, u=2),
+                in_=bank[:].rearrange("p (n u r) -> p n r u", r=P, u=2),
             )
             return t
 
         def copy_et(s):
-            engine_copy = nc.vector.tensor_copy if STEPS - 1 > s >= VECTOR_COPY_FROM and (s - VECTOR_COPY_FROM + 1) % COPY_PERIOD else nc.scalar.copy
+            on_scalar = s % A_PERIOD == 0 if s < FIRST_UNIT_SLOT else s % B_PERIOD == 0
+            engine_copy = nc.scalar.copy if on_scalar or s == len(steps) - 1 else nc.vector.tensor_copy
             et_grouped[s] = copy_bank(engine_copy, et_bank[s], "et_grouped")
 
         def quantize_et(s):
-            codes = flow.tile([P, 2 * P], U32, name="et_codes", bufs=12, align_bytes=64)
-            scales = flow.tile([P, 2 * P], U8, name="et_scales", bufs=12, align_bytes=64)
+            i, passes = steps[s]
+            codes = flow.tile([P, len(passes) * P], U32, name="et_codes", bufs=12, align_bytes=64)
+            scales = flow.tile([P, len(passes) * P], U8, name="et_scales", bufs=12, align_bytes=64)
             nc.vector.quantize_mx(out=codes[:].bitcast(E5M2X4), scales=scales[:], in_=et_grouped[s][:])
-            et_codes[s] = codes
-            et_scales[s] = scales
+            for n, g in enumerate(passes):
+                et_codes[i, g] = codes[:, n * P : (n + 1) * P]
+                et_scales[i, g] = scales[:, n * P : (n + 1) * P]
 
         def acc_bank(j):
             return j if j < 6 else (0, 1, 4, 5)[(j - 6) % 4]
@@ -193,13 +207,11 @@ def tile_vision_momentum_sgd_step_b13_kernel(
             i, h = divmod(j, HALVES)
             if g == 0:
                 acc[j] = psum.tile([P, HALF], F32, name="acc", tag="bank%d" % acc_bank(j), bufs=1)
-            s = STEPS_PER_TILE * i + g // 2
-            cols = slice((g % 2) * P, (g % 2 + 1) * P)
             c = HALVES * g + h
             nc.tensor.matmul_mx(
                 out=acc[j][:],
-                lhsT=et_codes[s][:, cols].bitcast(E5M2X4),
-                lhsT_scale=et_scales[s][:, cols],
+                lhsT=et_codes[i, g].bitcast(E5M2X4),
+                lhsT_scale=et_scales[i, g],
                 rhs=a_codes[c][:].bitcast(E4M3X4),
                 rhs_scale=a_scales[c][:],
                 start=(g == 0),
@@ -212,6 +224,14 @@ def tile_vision_momentum_sgd_step_b13_kernel(
         y_grouped = {}
         y_codes = {}
         y_scales = keep.tile([P, HALVES * 2 * N], U8, align_bytes=64)
+
+        def store_y(j, parts):
+            i, h = divmod(j, HALVES)
+            rows = out_0[parts.start : parts.stop, i * P : (i + 1) * P, h * HALF : (h + 1) * HALF]
+            nc.sync.dma_start(
+                out=rows.rearrange("s p k -> p s k"),
+                in_=y[j][:, parts.start * HALF : parts.stop * HALF].rearrange("p (s k) -> p s k", k=HALF),
+            )
 
         def new_momentum(j):
             i, h = divmod(j, HALVES)
@@ -229,71 +249,75 @@ def tile_vision_momentum_sgd_step_b13_kernel(
                 out=y[j][:, HALF : 2 * HALF], in0=y[j][:, 0:HALF], scalar=neg_rate[:, i : i + 1],
                 in1=w_old[i][:, h * HALF : (h + 1) * HALF], op0=MULT, op1=ADD,
             )
-            nc.sync.dma_start(
-                out=out_0[:, i * P : (i + 1) * P, h * HALF : (h + 1) * HALF].rearrange("s p k -> p s k"),
-                in_=y[j][:].rearrange("p (s k) -> p s k", s=2),
-            )
 
-        def round_y(j, engine_copy):
-            t = flow.tile([P, 2 * HALF], BF16, name="y_sorted", bufs=4)
+        def round_y(j, parts, engine_copy):
+            t = flow.tile([P, len(parts) * HALF], BF16, name="y_sorted", bufs=4)
             engine_copy(
                 out=t[:].rearrange("p (u q e) -> p u q e", u=2, e=2),
-                in_=y[j][:].rearrange("p (q u e) -> p u q e", u=2, e=2),
+                in_=y[j][:, parts.start * HALF : parts.stop * HALF].rearrange("p (q u e) -> p u q e", u=2, e=2),
             )
-            y_sorted[j] = t
+            y_sorted[j, parts] = t
 
-        def turn_y(j):
-            bank = psum.tile([P, 4 * P], F32, name="y_bank", tag="bank%d" % (2 + j % 2), bufs=1)
-            pairs = y_sorted[j][:].bitcast(F32)
-            for s in range(2):
+        def turn_y(j, parts, bank_number):
+            count = len(parts)
+            bank = psum.tile([P, count * 2 * P], F32, name="y_bank", tag="bank%d" % bank_number, bufs=1)
+            pairs = y_sorted[j, parts][:].bitcast(F32)
+            for n in range(count):
                 for u in range(2):
                     nc.tensor.transpose(
-                        bank[:, (2 * s + u) * P : (2 * s + u + 1) * P],
-                        pairs[:, (2 * u + s) * P : (2 * u + s + 1) * P],
+                        bank[:, (2 * n + u) * P : (2 * n + u + 1) * P],
+                        pairs[:, (count * u + n) * P : (count * u + n + 1) * P],
                         ident[:],
                     )
-            y_bank[j] = bank
+            y_bank[j, parts] = bank
 
-        def copy_y(j):
-            y_grouped[j] = copy_bank(nc.scalar.copy, y_bank[j], "y_grouped")
+        def copy_y(j, parts):
+            y_grouped[j, parts] = copy_bank(nc.scalar.copy, y_bank[j, parts], "y_grouped")
 
-        def quantize_y(j):
+        code_groups = [range(0, 2), range(2, 4), range(4, 7), range(7, 8)]
+
+        def quantize_y(j, parts):
             i, h = divmod(j, HALVES)
-            pair, second = divmod(i, 2)
-            if second == 0:
-                y_codes[pair, h] = flow.tile([P, 4 * P], U32, name="y_codes", bufs=6, align_bytes=64)
-            codes = y_codes[pair, h]
-            for s in range(2):
+            group = [tiles for tiles in code_groups if i in tiles][0]
+            width = len(group) * P
+            if (group, h) not in y_codes:
+                y_codes[group, h] = flow.tile([P, 2 * width], U32, name="y_codes", bufs=6, align_bytes=64)
+            codes = y_codes[group, h]
+            for n, s in enumerate(parts):
+                first = s * width + (i - group.start) * P
                 nc.vector.quantize_mx(
-                    out=codes[:, (2 * s + second) * P : (2 * s + second + 1) * P].bitcast(E4M3X4),
+                    out=codes[:, first : first + P].bitcast(E4M3X4),
                     scales=y_scales[:, (2 * h + s) * N + i * P : (2 * h + s) * N + (i + 1) * P],
-                    in_=y_grouped[j][:, s * PASS : (s + 1) * PASS],
+                    in_=y_grouped[j, parts][:, n * PASS : (n + 1) * PASS],
                 )
-            if second == 1:
+            if i == group.stop - 1 and parts.stop == 2:
                 nc.sync.dma_start(
-                    out=words_out[h].rearrange("p (s n) -> p s n", s=2)[:, :, 2 * pair * P : 2 * (pair + 1) * P],
+                    out=words_out[h].rearrange("p (s n) -> p s n", s=2)[:, :, group.start * P : group.stop * P],
                     in_=codes[:].bitcast(I32).rearrange("p (s n) -> p s n", s=2),
                 )
-            if j == UNITS - 1:
-                for q in range(4):
-                    (nc.sync, nc.scalar)[q % 2].dma_start(
-                        out=scales_out[:, 4 * q : 4 * q + 4, :].rearrange("h r m -> r h m"),
-                        in_=y_scales[32 * q : 32 * q + 4, :].bitcast(I32).rearrange("r (h m) -> r h m", h=HALVES),
-                    )
+
+        def store_scales():
+            for q in range(4):
+                (nc.scalar, nc.sync)[q % 2].dma_start(
+                    out=scales_out[:, 4 * q : 4 * q + 4, :].rearrange("h r m -> r h m"),
+                    in_=y_scales[32 * q : 32 * q + 4, :].bitcast(I32).rearrange("r (h m) -> r h m", h=HALVES),
+                )
+
+        both, mom_part, w_part = range(0, 2), range(0, 1), range(1, 2)
 
         load_scales(0, 1)
-        load_et(0, 0, 1, "et_first", 1)
+        load_et(0, 0, 2, "et_first", 1)
         load_a(0)
-        load_et(0, 1, STEPS_PER_TILE, "et_second", 1)
+        load_et(0, 2, PASSES, "et_second", 1)
         load_a(1)
         load_scales(1, TILES - 1)
         load_a(2)
         load_a(3)
-        load_et(1, 0, STEPS_PER_TILE, "et_bytes", 4)
+        load_et(1, 0, PASSES, "et_bytes", 4)
         load_a(4)
         load_a(5)
         load_rate()
-        load_et(2, 0, STEPS_PER_TILE, "et_bytes", 4)
+        load_et(2, 0, PASSES, "et_bytes", 4)
         load_a(6)
         load_a(7)
 
@@ -303,21 +327,21 @@ def tile_vision_momentum_sgd_step_b13_kernel(
                 load_state(0)
             if slot == 3:
                 load_a(9)
-                load_et(3, 0, STEPS_PER_TILE, "et_bytes", 4)
+                load_et(3, 0, PASSES, "et_bytes", 4)
             if slot == 4:
                 load_a(10)
-                load_et(4, 0, STEPS_PER_TILE, "et_bytes", 4)
+                load_et(4, 0, PASSES, "et_bytes", 4)
             if slot == 5:
                 load_a(11)
                 load_state(1)
             if slot == 6:
-                load_et(5, 0, STEPS_PER_TILE, "et_bytes", 4)
+                load_et(5, 0, PASSES, "et_bytes", 4)
                 load_state(2)
                 load_state(3)
             if slot == 9:
-                load_et(6, 0, STEPS_PER_TILE, "et_bytes", 4)
+                load_et(6, 0, PASSES, "et_bytes", 4)
             if slot == 12:
-                load_et(7, 0, STEPS_PER_TILE, "et_bytes", 4)
+                load_et(7, 0, PASSES, "et_bytes", 4)
 
         def within(index, count):
             return 0 <= index < count
@@ -326,9 +350,9 @@ def tile_vision_momentum_sgd_step_b13_kernel(
 
         def ready(j, g, slot):
             i, h = divmod(j, HALVES)
-            et_done = STEPS_PER_TILE * i + g // 2 + 2 <= slot
+            et_done = step_of[i, g] + ET_LAG <= slot
             a_done = chunk_slot[HALVES * g + h] + (2 if g < A_LAG else 1) <= slot
-            bank_free = j < 6 or FIRST_UNIT_SLOT + bank_before(j) <= slot
+            bank_free = j < 6 or FIRST_UNIT_SLOT + bank_before(j) + BANK_LAG <= slot
             return et_done and a_done and bank_free and slot >= MM_START
 
         interleaved = []
@@ -342,9 +366,9 @@ def tile_vision_momentum_sgd_step_b13_kernel(
             if within(j, UNITS):
                 new_momentum(j)
             if within(j - 1, UNITS):
-                round_y(j - 1, nc.vector.tensor_copy)
+                round_y(j - 1, both, nc.vector.tensor_copy)
             if within(j - T_LAG, UNITS):
-                turn_y(j - T_LAG)
+                turn_y(j - T_LAG, both, 2 + j % 2)
             if within(slot, STEPS):
                 widen(slot)
             chunks = [c for c in range(CHUNKS) if chunk_slot[c] == slot]
@@ -356,63 +380,75 @@ def tile_vision_momentum_sgd_step_b13_kernel(
             if not chunks and interleaved:
                 quantize_a(interleaved.pop())
             if within(j - Y_LAG, UNITS):
-                quantize_y(j - Y_LAG)
+                quantize_y(j - Y_LAG, both)
             if within(j, UNITS):
                 new_weights(j)
+                store_y(j, both)
             if within(slot - 2, STEPS):
                 quantize_et(slot - 2)
             if within(slot - 1, STEPS):
                 copy_et(slot - 1)
             if within(j - T_LAG, UNITS):
-                copy_y(j - T_LAG)
+                copy_y(j - T_LAG, both)
             waiting = [(unit, g) for unit in range(UNITS) for g in range(PASSES) if (unit, g) not in done]
-            for unit, g in [x for x in waiting if ready(x[0], x[1], slot)][: MM_CAP if CAP_FROM <= j and slot < STEPS else None]:
+            for unit, g in [x for x in waiting if ready(x[0], x[1], slot)][: MM_CAP if slot < STEPS - 1 else CAP_LAST]:
                 multiply(unit, g)
                 done.add((unit, g))
 
-        def multiply_rest(passes):
-            for unit in range(UNITS):
-                for g in range(passes):
-                    if (unit, g) not in done:
-                        multiply(unit, g)
-                        done.add((unit, g))
+        def multiply_some(unit, passes):
+            for g in range(passes):
+                if (unit, g) not in done:
+                    multiply(unit, g)
+                    done.add((unit, g))
 
         assert FIRST_UNIT_SLOT == 12
+        V, S = nc.vector.tensor_copy, nc.scalar.copy
         turn_et(23)
-        turn_y(10)
-        quantize_et(22)
-        multiply_rest(4)
-        round_y(11, nc.scalar.copy)
-        copy_et(23)
-        copy_y(10)
+        turn_y(10, both, 2)
+        widen(24)
+        multiply_some(13, 6)
+        multiply_some(14, 2)
+        multiply_some(15, 2)
         new_momentum(12)
-        quantize_y(9)
+        quantize_et(22)
+        copy_et(23)
+        turn_et(24)
+        multiply_some(14, 4)
+        multiply_some(15, 4)
         new_weights(12)
+        store_y(12, both)
         quantize_et(23)
-        multiply_rest(6)
-        turn_y(11)
-        round_y(12, nc.scalar.copy)
-        copy_y(11)
+        copy_y(10, both)
+        copy_et(24)
+        round_y(11, both, S)
         new_momentum(13)
-        quantize_y(10)
+        quantize_et(24)
+        multiply_some(14, 6)
+        multiply_some(15, 6)
+        turn_y(11, both, 3)
         new_weights(13)
-        turn_y(12)
-        round_y(13, nc.scalar.copy)
-        copy_y(12)
+        store_y(13, both)
+        quantize_y(9, both)
+        quantize_y(10, both)
+        round_y(12, both, S)
+        turn_y(12, both, 2)
+        copy_y(11, both)
+        round_y(13, both, S)
+        turn_y(13, both, 3)
+        copy_y(12, both)
         new_momentum(14)
         new_momentum(15)
         new_weights(14)
+        store_y(14, both)
         new_weights(15)
-        turn_y(13)
-        copy_y(13)
-        round_y(14, nc.vector.tensor_copy)
-        round_y(15, nc.vector.tensor_copy)
-        turn_y(14)
-        copy_y(14)
-        turn_y(15)
-        copy_y(15)
-        quantize_y(11)
-        quantize_y(12)
-        quantize_y(13)
-        quantize_y(14)
-        quantize_y(15)
+        store_y(15, both)
+        round_y(14, both, V)
+        round_y(15, both, V)
+        turn_y(14, both, 4)
+        turn_y(15, both, 5)
+        copy_y(13, both)
+        copy_y(14, both)
+        copy_y(15, both)
+        for j in range(11, 16):
+            quantize_y(j, both)
+        store_scales()

@@ -37,12 +37,14 @@ A_SLOTS = 12
 A_LAG = 4
 FIRST_UNIT_SLOT = 12
 MM_CAP = 5
-MM_START = 5
-A_PERIOD = 2
+MM_START = 6
+RING = (0, 1, 4, 5)
+Y_BANKS = (2, 3)
+A_PERIOD = 1
 ET_LAG = 2
 BANK_LAG = 0
-B_PERIOD = 4
-CAP_LAST = 0
+B_PERIOD = 2
+CAP_LAST = 2
 CAP_FROM = -20
 T_LAG = 2
 Y_LAG = 3
@@ -93,28 +95,26 @@ def tile_vision_momentum_sgd_step_b13_kernel(
             for g in range(g0, g1):
                 et_bytes[i, g] = t[:, (g - g0) * PASS : (g - g0 + 1) * PASS]
 
-        def load_a(c):
-            g, h = divmod(c, HALVES)
-            t = flow.tile([P, PACK, HALF], BF16, name="a_raw", bufs=8)
-            rows = A[g * PASS : (g + 1) * PASS, h * HALF : (h + 1) * HALF]
+        def load_a(g, halves, name, bufs):
+            t = flow.tile([P, PACK, len(halves) * HALF], BF16, name=name, bufs=bufs)
+            rows = A[g * PASS : (g + 1) * PASS, halves.start * HALF : halves.stop * HALF]
             nc.sync.dma_start(out=t[:], in_=rows.rearrange("(p j) k -> p j k", j=PACK))
-            a_raw[c] = t
+            for n, h in enumerate(halves):
+                a_raw[HALVES * g + h] = t[:, :, n * HALF : (n + 1) * HALF]
 
-        def load_state(pair):
-            for src, dst, name in ((Mom, mom_old, "mom_old%d"), (W, w_old, "w_old%d")):
-                t = keep.tile([P, 2, K], BF16, name=name % pair)
-                rows = src[2 * pair * P : 2 * (pair + 1) * P, :]
-                nc.sync.dma_start(out=t[:], in_=rows.rearrange("(i p) k -> p i k", p=P))
-                for i in range(2):
-                    dst[2 * pair + i] = t[:, i, :]
+        def load_state(i):
+            for src, dst, name in ((Mom, mom_old, "mom_old"), (W, w_old, "w_old")):
+                t = flow.tile([P, K], BF16, name=name, bufs=4)
+                nc.sync.dma_start(out=t[:], in_=src[i * P : (i + 1) * P, :])
+                dst[i] = t
 
         def load_rate():
             nc.sync.dma_start(out=rate_rows[0:TILES, :], in_=rate.rearrange("(i p) o -> i (p o)", p=P))
 
         def make_neg_rate():
-            bank = psum.tile([P, P], BF16, name="et_bank")
+            bank = psum.tile([P, P], BF16, name="rate_bank", tag="bank5", bufs=1)
             nc.tensor.transpose(bank[:], rate_rows[:], ident_bf[:])
-            nc.scalar.activation(out=neg_rate[:], in_=bank[:, 0:TILES], func=COPY, scale=-1.0)
+            return bank
 
         a_grouped = {}
         a_codes = {}
@@ -124,7 +124,7 @@ def tile_vision_momentum_sgd_step_b13_kernel(
             t = flow.tile([P, HALF * PACK], BF16, name="a_grouped", bufs=2, align_bytes=64)
             nc.vector.tensor_copy(
                 out=t[:].rearrange("p (c i j) -> p c j i", i=4, j=PACK),
-                in_=a_raw[c][:].rearrange("p j (c i) -> p c j i", i=4),
+                in_=a_raw[c].rearrange("p j (c i) -> p c j i", i=4),
             )
             a_grouped[c] = t
 
@@ -195,7 +195,7 @@ def tile_vision_momentum_sgd_step_b13_kernel(
                 et_scales[i, g] = scales[:, n * P : (n + 1) * P]
 
         def acc_bank(j):
-            return j if j < 6 else (0, 1, 4, 5)[(j - 6) % 4]
+            return j if j < 6 else RING[(j - 6) % len(RING)]
 
         def bank_before(j):
             return max(x for x in range(j) if acc_bank(x) == acc_bank(j))
@@ -253,8 +253,8 @@ def tile_vision_momentum_sgd_step_b13_kernel(
         def round_y(j, parts, engine_copy):
             t = flow.tile([P, len(parts) * HALF], BF16, name="y_sorted", bufs=4)
             engine_copy(
-                out=t[:].rearrange("p (u q e) -> p u q e", u=2, e=2),
-                in_=y[j][:, parts.start * HALF : parts.stop * HALF].rearrange("p (q u e) -> p u q e", u=2, e=2),
+                out=t[:].rearrange("p (n u q e) -> p n u q e", u=2, q=P, e=2),
+                in_=y[j][:, parts.start * HALF : parts.stop * HALF].rearrange("p (n q u e) -> p n u q e", u=2, q=P, e=2),
             )
             y_sorted[j, parts] = t
 
@@ -266,7 +266,7 @@ def tile_vision_momentum_sgd_step_b13_kernel(
                 for u in range(2):
                     nc.tensor.transpose(
                         bank[:, (2 * n + u) * P : (2 * n + u + 1) * P],
-                        pairs[:, (count * u + n) * P : (count * u + n + 1) * P],
+                        pairs[:, (2 * n + u) * P : (2 * n + u + 1) * P],
                         ident[:],
                     )
             y_bank[j, parts] = bank
@@ -306,42 +306,31 @@ def tile_vision_momentum_sgd_step_b13_kernel(
         both, mom_part, w_part = range(0, 2), range(0, 1), range(1, 2)
 
         load_scales(0, 1)
-        load_et(0, 0, 2, "et_first", 1)
-        load_a(0)
-        load_et(0, 2, PASSES, "et_second", 1)
-        load_a(1)
+        load_et(0, 0, 2, "et_first", 3)
+        load_a(0, range(0, 1), "a_first", 2)
+        load_et(0, 2, 4, "et_first", 3)
+        load_a(0, range(1, 2), "a_first", 2)
+        load_et(0, 4, 6, "et_first", 3)
+        load_a(1, range(HALVES), "a_raw", 5)
         load_scales(1, TILES - 1)
-        load_a(2)
-        load_a(3)
-        load_et(1, 0, PASSES, "et_bytes", 4)
-        load_a(4)
-        load_a(5)
+        load_et(1, 0, PASSES, "et_bytes", 7)
         load_rate()
-        load_et(2, 0, PASSES, "et_bytes", 4)
-        load_a(6)
-        load_a(7)
+        load_a(2, range(HALVES), "a_raw", 5)
+        load_a(3, range(HALVES), "a_raw", 5)
+        load_et(2, 0, PASSES, "et_bytes", 7)
+        load_a(4, range(HALVES), "a_raw", 5)
+        load_et(3, 0, PASSES, "et_bytes", 7)
+        load_a(5, range(HALVES), "a_raw", 5)
+        load_state(0)
+        for i in range(4, TILES):
+            load_et(i, 0, PASSES, "et_bytes", 7)
+            if i < TILES - 1:
+                load_state(i - 3)
 
         def late_loads(slot):
-            if slot == 2:
-                load_a(8)
-                load_state(0)
-            if slot == 3:
-                load_a(9)
-                load_et(3, 0, PASSES, "et_bytes", 4)
-            if slot == 4:
-                load_a(10)
-                load_et(4, 0, PASSES, "et_bytes", 4)
-            if slot == 5:
-                load_a(11)
-                load_state(1)
-            if slot == 6:
-                load_et(5, 0, PASSES, "et_bytes", 4)
-                load_state(2)
-                load_state(3)
-            if slot == 9:
-                load_et(6, 0, PASSES, "et_bytes", 4)
-            if slot == 12:
-                load_et(7, 0, PASSES, "et_bytes", 4)
+            j = slot - FIRST_UNIT_SLOT
+            if j >= 2 and j % 2 == 0 and j // 2 + 3 < TILES:
+                load_state(j // 2 + 3)
 
         def within(index, count):
             return 0 <= index < count
@@ -359,8 +348,10 @@ def tile_vision_momentum_sgd_step_b13_kernel(
         for slot in range(STEPS):
             j = slot - FIRST_UNIT_SLOT
             late_loads(slot)
-            if slot == 8:
-                make_neg_rate()
+            if slot == 6:
+                rate_bank = make_neg_rate()
+            if slot == 7:
+                nc.scalar.activation(out=neg_rate[:], in_=rate_bank[:, 0:TILES], func=COPY, scale=-1.0)
             if within(slot - 1, STEPS):
                 turn_et(slot - 1)
             if within(j, UNITS):
@@ -368,7 +359,7 @@ def tile_vision_momentum_sgd_step_b13_kernel(
             if within(j - 1, UNITS):
                 round_y(j - 1, both, nc.vector.tensor_copy)
             if within(j - T_LAG, UNITS):
-                turn_y(j - T_LAG, both, 2 + j % 2)
+                turn_y(j - T_LAG, both, Y_BANKS[j % 2])
             if within(slot, STEPS):
                 widen(slot)
             chunks = [c for c in range(CHUNKS) if chunk_slot[c] == slot]
@@ -404,7 +395,7 @@ def tile_vision_momentum_sgd_step_b13_kernel(
         assert FIRST_UNIT_SLOT == 12
         V, S = nc.vector.tensor_copy, nc.scalar.copy
         turn_et(23)
-        turn_y(10, both, 2)
+        turn_y(10, both, Y_BANKS[0])
         widen(24)
         multiply_some(13, 6)
         multiply_some(14, 2)
@@ -425,16 +416,16 @@ def tile_vision_momentum_sgd_step_b13_kernel(
         quantize_et(24)
         multiply_some(14, 6)
         multiply_some(15, 6)
-        turn_y(11, both, 3)
+        turn_y(11, both, Y_BANKS[1])
         new_weights(13)
         store_y(13, both)
         quantize_y(9, both)
         quantize_y(10, both)
         round_y(12, both, S)
-        turn_y(12, both, 2)
+        turn_y(12, both, acc_bank(12))
         copy_y(11, both)
         round_y(13, both, S)
-        turn_y(13, both, 3)
+        turn_y(13, both, acc_bank(13))
         copy_y(12, both)
         new_momentum(14)
         new_momentum(15)
@@ -444,8 +435,8 @@ def tile_vision_momentum_sgd_step_b13_kernel(
         store_y(15, both)
         round_y(14, both, V)
         round_y(15, both, V)
-        turn_y(14, both, 4)
-        turn_y(15, both, 5)
+        turn_y(14, both, acc_bank(14))
+        turn_y(15, both, acc_bank(15))
         copy_y(13, both)
         copy_y(14, both)
         copy_y(15, both)

@@ -3,7 +3,8 @@ from contextlib import ExitStack
 import concourse.mybir as mybir
 from concourse.masks import make_identity
 
-T, N, K, B = 3072, 1024, 1024, 32
+T, N, K = 3072, 1024, 1024
+BLOCK = 32
 MU = 0.9
 FLOPS = 2 * T * N * K
 
@@ -26,37 +27,28 @@ PASSES = T // PASS
 HALF = 512
 HALVES = K // HALF
 TILES = N // P
-STEP = 2 * PASS
-STEPS_PER_TILE = T // STEP
-STEPS = TILES * STEPS_PER_TILE
 CHUNKS = PASSES * HALVES
 UNITS = TILES * HALVES
+RESULTS = 2
+SLOTS = T * TILES // (2 * PASS)
 
-ACC_BANKS = 4
-A_SLOTS = 12
-A_LAG = 4
-FIRST_UNIT_SLOT = 12
-MM_CAP = 5
-MM_START = 6
-RING = (0, 1, 4, 5)
-Y_BANKS = (2, 3)
-A_PERIOD = 1
-ET_LAG = 2
-BANK_LAG = 0
-B_PERIOD = 2
-CAP_LAST = 2
-CAP_FROM = -20
-T_LAG = 2
-Y_LAG = 3
-COPY_PERIOD = 2
-VECTOR_COPY_FROM = 10
-SCALAR_CAST_FROM = 12
+NUMBERED_BANKS = 6
+RESULT_BANKS = (2, 3)
+RING_BANKS = (0, 1, 4, 5)
+
+FIRST_UNIT_SLOT = CHUNKS
+VECTOR_COPY_STEPS = range(10, 18)
+FIRST_MATMUL_SLOT = 6
+MATMULS_PER_SLOT = 5
+STEP_TO_MATMUL = 3
+CHUNK_TO_MATMUL = 2
 
 
 def tile_vision_momentum_sgd_step_b13_kernel(
     tc, Et_bytes, Et_scale, A, Mom, W, rate, out_0, out_1, out_2
 ):
     nc = tc.nc
+    on_vector, on_scalar = nc.vector.tensor_copy, nc.scalar.copy
     words_out = out_1.rearrange("g p m t -> g p (m t)").bitcast(I32)
     scales_out = out_2.bitcast(I32)
 
@@ -70,61 +62,66 @@ def tile_vision_momentum_sgd_step_b13_kernel(
         make_identity(nc, ident[:])
         rate_rows = keep.tile([P, P], BF16)
         nc.gpsimd.memset(rate_rows[:], 0.0)
-        ident_bf = keep.tile([P, P], BF16)
-        make_identity(nc, ident_bf[:])
+        ident_bf16 = keep.tile([P, P], BF16)
+        make_identity(nc, ident_bf16[:])
         neg_rate = keep.tile([P, TILES], F32)
 
-        et_scale = {}
-        et_bytes = {}
-        a_raw = {}
-        mom_old = {}
-        w_old = {}
+        def numbered_bank(number, shape, dtype):
+            return psum.tile(shape, dtype, name="numbered", tag="bank%d" % number, bufs=1)
 
-        def load_scales(first, count):
-            t = keep.tile([P, count * (T // B)], F32, name="et_scale%d" % first)
+        et_scale, et_bytes, a_raw, mom_old, w_old = {}, {}, {}, {}, {}
+
+        def load_scales(tiles):
+            blocks = T // BLOCK
+            t = keep.tile([P, len(tiles) * blocks], F32, name="et_scale%d" % tiles.start)
             nc.sync.dma_start(
-                out=t[:].rearrange("p (i b) -> p i b", i=count),
-                in_=Et_scale[first * P : (first + count) * P, :].rearrange("(i p) b -> p i b", p=P),
+                out=t[:].rearrange("p (i b) -> p i b", b=blocks),
+                in_=Et_scale[tiles.start * P : tiles.stop * P, :].rearrange("(i p) b -> p i b", p=P),
             )
-            for i in range(count):
-                et_scale[first + i] = t[:, i * (T // B) : (i + 1) * (T // B)]
+            for n, i in enumerate(tiles):
+                et_scale[i] = t[:, n * blocks : (n + 1) * blocks]
 
-        def load_et(i, g0, g1, name, bufs):
-            t = flow.tile([P, (g1 - g0) * PASS], U8, name=name, bufs=bufs)
-            nc.sync.dma_start(out=t[:], in_=Et_bytes[i * P : (i + 1) * P, g0 * PASS : g1 * PASS])
-            for g in range(g0, g1):
-                et_bytes[i, g] = t[:, (g - g0) * PASS : (g - g0 + 1) * PASS]
+        def load_et(i, passes, name, bufs):
+            t = flow.tile([P, len(passes) * PASS], U8, name=name, bufs=bufs)
+            nc.sync.dma_start(out=t[:], in_=Et_bytes[i * P : (i + 1) * P, passes.start * PASS : passes.stop * PASS])
+            for n, g in enumerate(passes):
+                et_bytes[i, g] = t[:, n * PASS : (n + 1) * PASS]
 
-        def load_a(g, halves, name, bufs):
-            t = flow.tile([P, PACK, len(halves) * HALF], BF16, name=name, bufs=bufs)
+        def load_first_tile(step):
+            load_et(0, range(2 * step, 2 * step + 2), "et_first", 3)
+
+        def load_tile(i):
+            load_et(i, range(PASSES), "et_bytes", TILES - 1)
+
+        def load_a(g, halves, name):
+            t = flow.tile([P, PACK, len(halves) * HALF], BF16, name=name, bufs=4)
             rows = A[g * PASS : (g + 1) * PASS, halves.start * HALF : halves.stop * HALF]
-            nc.sync.dma_start(out=t[:], in_=rows.rearrange("(p j) k -> p j k", j=PACK))
+            nc.sync.dma_start(out=t[:], in_=rows.rearrange("(p t) k -> p t k", t=PACK))
             for n, h in enumerate(halves):
                 a_raw[HALVES * g + h] = t[:, :, n * HALF : (n + 1) * HALF]
 
+        def load_chunk(c):
+            g, h = divmod(c, HALVES)
+            load_a(g, range(h, h + 1), "a_first")
+
+        def load_pass(g):
+            load_a(g, range(HALVES), "a_raw")
+
+        state_tiles = 4
+
         def load_state(i):
             for src, dst, name in ((Mom, mom_old, "mom_old"), (W, w_old, "w_old")):
-                t = flow.tile([P, K], BF16, name=name, bufs=4)
+                t = flow.tile([P, K], BF16, name=name, bufs=state_tiles)
                 nc.sync.dma_start(out=t[:], in_=src[i * P : (i + 1) * P, :])
                 dst[i] = t
 
-        def load_rate():
-            nc.sync.dma_start(out=rate_rows[0:TILES, :], in_=rate.rearrange("(i p) o -> i (p o)", p=P))
-
-        def make_neg_rate():
-            bank = psum.tile([P, P], BF16, name="rate_bank", tag="bank5", bufs=1)
-            nc.tensor.transpose(bank[:], rate_rows[:], ident_bf[:])
-            return bank
-
-        a_grouped = {}
-        a_codes = {}
-        a_scales = {}
+        a_grouped, a_codes, a_scales = {}, {}, {}
 
         def interleave_a(c):
-            t = flow.tile([P, HALF * PACK], BF16, name="a_grouped", bufs=2, align_bytes=64)
+            t = flow.tile([P, HALF * PACK], BF16, name="a_grouped", align_bytes=64)
             nc.vector.tensor_copy(
-                out=t[:].rearrange("p (c i j) -> p c j i", i=4, j=PACK),
-                in_=a_raw[c].rearrange("p j (c i) -> p c j i", i=4),
+                out=t[:].rearrange("p (c i t) -> p c t i", i=4, t=PACK),
+                in_=a_raw[c].rearrange("p t (c i) -> p c t i", i=4),
             )
             a_grouped[c] = t
 
@@ -135,25 +132,20 @@ def tile_vision_momentum_sgd_step_b13_kernel(
             a_codes[c] = codes
             a_scales[c] = scales
 
-        et_wide = {}
-        et_bank = {}
-        et_grouped = {}
-        et_codes = {}
-        et_scales = {}
-
         steps = [(i, range(g, g + 2)) for i in range(TILES) for g in range(0, PASSES, 2)]
         steps = steps[:-1] + [(TILES - 1, range(g, g + 1)) for g in (PASSES - 2, PASSES - 1)]
         step_of = {(i, g): s for s, (i, passes) in enumerate(steps) for g in passes}
+        et_wide, et_bank, et_grouped, et_codes, et_scales = {}, {}, {}, {}, {}
 
         def widen(s):
             i, passes = steps[s]
             t = flow.tile([P, len(passes) * PASS], BF16, name="et_wide")
             for n, g in enumerate(passes):
-                for q in range(PASS // B):
-                    block = g * (PASS // B) + q
+                for q in range(PASS // BLOCK):
+                    block = g * (PASS // BLOCK) + q
                     nc.scalar.activation(
-                        out=t[:, n * PASS + q * B : n * PASS + (q + 1) * B],
-                        in_=et_bytes[i, g][:, q * B : (q + 1) * B].bitcast(FP8),
+                        out=t[:, n * PASS + q * BLOCK : n * PASS + (q + 1) * BLOCK],
+                        in_=et_bytes[i, g][:, q * BLOCK : (q + 1) * BLOCK].bitcast(FP8),
                         func=COPY,
                         scale=et_scale[i][:, block : block + 1],
                     )
@@ -173,7 +165,7 @@ def tile_vision_momentum_sgd_step_b13_kernel(
             et_bank[s] = bank
 
         def copy_bank(engine_copy, bank, name):
-            t = flow.tile([P, 2 * bank.shape[1]], BF16, name=name, bufs=7, align_bytes=64)
+            t = flow.tile([P, 2 * bank.shape[1]], BF16, name=name, bufs=8, align_bytes=64)
             engine_copy(
                 out=t[:].bitcast(F32).rearrange("p (n r u) -> p n r u", r=P, u=2),
                 in_=bank[:].rearrange("p (n u r) -> p n r u", r=P, u=2),
@@ -181,32 +173,27 @@ def tile_vision_momentum_sgd_step_b13_kernel(
             return t
 
         def copy_et(s):
-            on_scalar = s % A_PERIOD == 0 if s < FIRST_UNIT_SLOT else s % B_PERIOD == 0
-            engine_copy = nc.scalar.copy if on_scalar or s == len(steps) - 1 else nc.vector.tensor_copy
-            et_grouped[s] = copy_bank(engine_copy, et_bank[s], "et_grouped")
+            et_grouped[s] = copy_bank(on_vector if s in VECTOR_COPY_STEPS else on_scalar, et_bank[s], "et_grouped")
 
         def quantize_et(s):
             i, passes = steps[s]
-            codes = flow.tile([P, len(passes) * P], U32, name="et_codes", bufs=12, align_bytes=64)
-            scales = flow.tile([P, len(passes) * P], U8, name="et_scales", bufs=12, align_bytes=64)
+            codes = flow.tile([P, len(passes) * P], U32, name="et_codes", bufs=10, align_bytes=64)
+            scales = flow.tile([P, len(passes) * P], U8, name="et_scales", bufs=10, align_bytes=64)
             nc.vector.quantize_mx(out=codes[:].bitcast(E5M2X4), scales=scales[:], in_=et_grouped[s][:])
             for n, g in enumerate(passes):
                 et_codes[i, g] = codes[:, n * P : (n + 1) * P]
                 et_scales[i, g] = scales[:, n * P : (n + 1) * P]
 
-        def acc_bank(j):
-            return j if j < 6 else RING[(j - 6) % len(RING)]
-
-        def bank_before(j):
-            return max(x for x in range(j) if acc_bank(x) == acc_bank(j))
-
         acc = {}
-        done = set()
+        multiplied = set()
+
+        def acc_bank(j):
+            return j if j < NUMBERED_BANKS else RING_BANKS[(j - NUMBERED_BANKS) % len(RING_BANKS)]
 
         def multiply(j, g):
             i, h = divmod(j, HALVES)
             if g == 0:
-                acc[j] = psum.tile([P, HALF], F32, name="acc", tag="bank%d" % acc_bank(j), bufs=1)
+                acc[j] = numbered_bank(acc_bank(j), [P, HALF], F32)
             c = HALVES * g + h
             nc.tensor.matmul_mx(
                 out=acc[j][:],
@@ -217,13 +204,42 @@ def tile_vision_momentum_sgd_step_b13_kernel(
                 start=(g == 0),
                 stop=(g == PASSES - 1),
             )
+            multiplied.add((j, g))
 
-        y = {}
-        y_sorted = {}
-        y_bank = {}
-        y_grouped = {}
-        y_codes = {}
-        y_scales = keep.tile([P, HALVES * 2 * N], U8, align_bytes=64)
+        def multiply_up_to(units, passes):
+            for j in units:
+                for g in range(passes):
+                    if (j, g) not in multiplied:
+                        multiply(j, g)
+
+        both, mom_part, w_part = range(RESULTS), range(0, 1), range(1, 2)
+        y, y_sorted, y_bank, y_grouped, y_codes = {}, {}, {}, {}, {}
+        y_scales = keep.tile([P, HALVES * RESULTS * N], U8, align_bytes=64)
+
+        def new_momentum(j):
+            i, h = divmod(j, HALVES)
+            assert (j, PASSES - 1) in multiplied
+            t = flow.tile([P, RESULTS * HALF], F32, name="y", bufs=5)
+            nc.vector.scalar_tensor_tensor(
+                out=t[:, 0:HALF],
+                in0=mom_old[i][:, h * HALF : (h + 1) * HALF],
+                scalar=MU,
+                in1=acc[j][:],
+                op0=MULT,
+                op1=ADD,
+            )
+            y[j] = t
+
+        def new_weights(j):
+            i, h = divmod(j, HALVES)
+            nc.vector.scalar_tensor_tensor(
+                out=y[j][:, HALF : 2 * HALF],
+                in0=y[j][:, 0:HALF],
+                scalar=neg_rate[:, i : i + 1],
+                in1=w_old[i][:, h * HALF : (h + 1) * HALF],
+                op0=MULT,
+                op1=ADD,
+            )
 
         def store_y(j, parts):
             i, h = divmod(j, HALVES)
@@ -233,213 +249,184 @@ def tile_vision_momentum_sgd_step_b13_kernel(
                 in_=y[j][:, parts.start * HALF : parts.stop * HALF].rearrange("p (s k) -> p s k", k=HALF),
             )
 
-        def new_momentum(j):
-            i, h = divmod(j, HALVES)
-            assert (j, PASSES - 1) in done
-            t = flow.tile([P, 2 * HALF], F32, name="y", bufs=5)
-            nc.vector.scalar_tensor_tensor(
-                out=t[:, 0:HALF], in0=mom_old[i][:, h * HALF : (h + 1) * HALF], scalar=MU,
-                in1=acc[j][:], op0=MULT, op1=ADD,
-            )
-            y[j] = t
-
-        def new_weights(j):
-            i, h = divmod(j, HALVES)
-            nc.vector.scalar_tensor_tensor(
-                out=y[j][:, HALF : 2 * HALF], in0=y[j][:, 0:HALF], scalar=neg_rate[:, i : i + 1],
-                in1=w_old[i][:, h * HALF : (h + 1) * HALF], op0=MULT, op1=ADD,
-            )
-
         def round_y(j, parts, engine_copy):
             t = flow.tile([P, len(parts) * HALF], BF16, name="y_sorted", bufs=4)
             engine_copy(
                 out=t[:].rearrange("p (n u q e) -> p n u q e", u=2, q=P, e=2),
-                in_=y[j][:, parts.start * HALF : parts.stop * HALF].rearrange("p (n q u e) -> p n u q e", u=2, q=P, e=2),
+                in_=y[j][:, parts.start * HALF : parts.stop * HALF].rearrange(
+                    "p (n q u e) -> p n u q e", u=2, q=P, e=2
+                ),
             )
             y_sorted[j, parts] = t
 
         def turn_y(j, parts, bank_number):
-            count = len(parts)
-            bank = psum.tile([P, count * 2 * P], F32, name="y_bank", tag="bank%d" % bank_number, bufs=1)
+            bank = numbered_bank(bank_number, [P, len(parts) * 2 * P], F32)
             pairs = y_sorted[j, parts][:].bitcast(F32)
-            for n in range(count):
-                for u in range(2):
-                    nc.tensor.transpose(
-                        bank[:, (2 * n + u) * P : (2 * n + u + 1) * P],
-                        pairs[:, (2 * n + u) * P : (2 * n + u + 1) * P],
-                        ident[:],
-                    )
+            for run in range(len(parts) * 2):
+                nc.tensor.transpose(bank[:, run * P : (run + 1) * P], pairs[:, run * P : (run + 1) * P], ident[:])
             y_bank[j, parts] = bank
 
         def copy_y(j, parts):
-            y_grouped[j, parts] = copy_bank(nc.scalar.copy, y_bank[j, parts], "y_grouped")
+            y_grouped[j, parts] = copy_bank(on_scalar, y_bank[j, parts], "y_grouped")
 
-        code_groups = [range(0, 2), range(2, 4), range(4, 7), range(7, 8)]
+        code_groups = [range(i, i + 2) for i in range(0, TILES - 2, 2)]
+        code_groups = code_groups + [range(i, i + 1) for i in (TILES - 2, TILES - 1)]
 
         def quantize_y(j, parts):
             i, h = divmod(j, HALVES)
             group = [tiles for tiles in code_groups if i in tiles][0]
             width = len(group) * P
             if (group, h) not in y_codes:
-                y_codes[group, h] = flow.tile([P, 2 * width], U32, name="y_codes", bufs=6, align_bytes=64)
+                y_codes[group, h] = flow.tile([P, RESULTS * width], U32, name="y_codes", bufs=6, align_bytes=64)
             codes = y_codes[group, h]
             for n, s in enumerate(parts):
-                first = s * width + (i - group.start) * P
+                first_code = s * width + (i - group.start) * P
+                first_scale = (RESULTS * h + s) * N + i * P
                 nc.vector.quantize_mx(
-                    out=codes[:, first : first + P].bitcast(E4M3X4),
-                    scales=y_scales[:, (2 * h + s) * N + i * P : (2 * h + s) * N + (i + 1) * P],
+                    out=codes[:, first_code : first_code + P].bitcast(E4M3X4),
+                    scales=y_scales[:, first_scale : first_scale + P],
                     in_=y_grouped[j, parts][:, n * PASS : (n + 1) * PASS],
                 )
-            if i == group.stop - 1 and parts.stop == 2:
+            if i == group.stop - 1 and parts.stop == RESULTS:
+                columns = words_out[h].rearrange("p (s n) -> p s n", s=RESULTS)
                 nc.sync.dma_start(
-                    out=words_out[h].rearrange("p (s n) -> p s n", s=2)[:, :, group.start * P : group.stop * P],
-                    in_=codes[:].bitcast(I32).rearrange("p (s n) -> p s n", s=2),
+                    out=columns[:, :, group.start * P : group.stop * P],
+                    in_=codes[:].bitcast(I32).rearrange("p (s n) -> p s n", s=RESULTS),
                 )
 
         def store_scales():
-            for q in range(4):
+            for q in range(P // 32):
                 (nc.scalar, nc.sync)[q % 2].dma_start(
                     out=scales_out[:, 4 * q : 4 * q + 4, :].rearrange("h r m -> r h m"),
                     in_=y_scales[32 * q : 32 * q + 4, :].bitcast(I32).rearrange("r (h m) -> r h m", h=HALVES),
                 )
 
-        both, mom_part, w_part = range(0, 2), range(0, 1), range(1, 2)
+        load_scales(range(0, 1))
+        for n in range(PASSES // 2):
+            load_first_tile(n)
+            load_chunk(n)
+        load_chunk(PASSES // 2)
+        load_scales(range(1, 2))
+        load_tile(1)
+        load_pass(2)
+        nc.sync.dma_start(out=rate_rows[0:TILES, :], in_=rate.rearrange("(i p) o -> i (p o)", p=P))
+        load_scales(range(2, TILES))
+        load_pass(3)
+        load_tile(2)
+        load_pass(4)
+        load_tile(3)
+        load_pass(5)
+        for i in range(state_tiles):
+            load_state(i)
+            load_tile(TILES - state_tiles + i)
 
-        load_scales(0, 1)
-        load_et(0, 0, 2, "et_first", 3)
-        load_a(0, range(0, 1), "a_first", 2)
-        load_et(0, 2, 4, "et_first", 3)
-        load_a(0, range(1, 2), "a_first", 2)
-        load_et(0, 4, 6, "et_first", 3)
-        load_a(1, range(HALVES), "a_raw", 5)
-        load_scales(1, TILES - 1)
-        load_et(1, 0, PASSES, "et_bytes", 7)
-        load_rate()
-        load_a(2, range(HALVES), "a_raw", 5)
-        load_a(3, range(HALVES), "a_raw", 5)
-        load_et(2, 0, PASSES, "et_bytes", 7)
-        load_a(4, range(HALVES), "a_raw", 5)
-        load_et(3, 0, PASSES, "et_bytes", 7)
-        load_a(5, range(HALVES), "a_raw", 5)
-        load_state(0)
-        for i in range(4, TILES):
-            load_et(i, 0, PASSES, "et_bytes", 7)
-            if i < TILES - 1:
-                load_state(i - 3)
-
-        def late_loads(slot):
-            j = slot - FIRST_UNIT_SLOT
-            if j >= 2 and j % 2 == 0 and j // 2 + 3 < TILES:
-                load_state(j // 2 + 3)
-
-        def within(index, count):
-            return 0 <= index < count
-
-        chunk_slot = [c * A_SLOTS // CHUNKS for c in range(CHUNKS)]
+        chunk_slot = [max(c - 1, 0) for c in range(CHUNKS)]
 
         def ready(j, g, slot):
             i, h = divmod(j, HALVES)
-            et_done = step_of[i, g] + ET_LAG <= slot
-            a_done = chunk_slot[HALVES * g + h] + (2 if g < A_LAG else 1) <= slot
-            bank_free = j < 6 or FIRST_UNIT_SLOT + bank_before(j) + BANK_LAG <= slot
-            return et_done and a_done and bank_free and slot >= MM_START
+            earlier = [x for x in range(j) if acc_bank(x) == acc_bank(j)]
+            bank_free = not earlier or FIRST_UNIT_SLOT + earlier[-1] <= slot
+            step_done = step_of[i, g] + STEP_TO_MATMUL <= slot
+            chunk_done = chunk_slot[HALVES * g + h] + CHUNK_TO_MATMUL <= slot
+            return bank_free and step_done and chunk_done
 
+        rate_bank = numbered_bank(NUMBERED_BANKS - 1, [P, P], BF16)
         interleaved = []
-        for slot in range(STEPS):
+        for slot in range(SLOTS):
             j = slot - FIRST_UNIT_SLOT
-            late_loads(slot)
-            if slot == 6:
-                rate_bank = make_neg_rate()
-            if slot == 7:
+            if j >= HALVES and j % HALVES == 0 and j // HALVES - 1 + state_tiles < TILES:
+                load_state(j // HALVES - 1 + state_tiles)
+            if slot == FIRST_MATMUL_SLOT:
+                nc.tensor.transpose(rate_bank[:], rate_rows[:], ident_bf16[:])
+            if slot == FIRST_MATMUL_SLOT + 1:
                 nc.scalar.activation(out=neg_rate[:], in_=rate_bank[:, 0:TILES], func=COPY, scale=-1.0)
-            if within(slot - 1, STEPS):
+            if slot >= 1:
                 turn_et(slot - 1)
-            if within(j, UNITS):
+            if j >= 0:
                 new_momentum(j)
-            if within(j - 1, UNITS):
-                round_y(j - 1, both, nc.vector.tensor_copy)
-            if within(j - T_LAG, UNITS):
-                turn_y(j - T_LAG, both, Y_BANKS[j % 2])
-            if within(slot, STEPS):
-                widen(slot)
+            if j >= 1:
+                round_y(j - 1, both, on_vector)
+            if j >= 2:
+                turn_y(j - 2, both, RESULT_BANKS[j % 2])
+            widen(slot)
             chunks = [c for c in range(CHUNKS) if chunk_slot[c] == slot]
             for c in chunks:
                 interleave_a(c)
                 if interleaved:
                     quantize_a(interleaved.pop())
                 interleaved.append(c)
-            if not chunks and interleaved:
+            if interleaved and not chunks:
                 quantize_a(interleaved.pop())
-            if within(j - Y_LAG, UNITS):
-                quantize_y(j - Y_LAG, both)
-            if within(j, UNITS):
+            if j >= 3:
+                quantize_y(j - 3, both)
+            if j >= 0:
                 new_weights(j)
                 store_y(j, both)
-            if within(slot - 2, STEPS):
+            if slot >= 2:
                 quantize_et(slot - 2)
-            if within(slot - 1, STEPS):
+            if slot >= 1:
                 copy_et(slot - 1)
-            if within(j - T_LAG, UNITS):
-                copy_y(j - T_LAG, both)
-            waiting = [(unit, g) for unit in range(UNITS) for g in range(PASSES) if (unit, g) not in done]
-            for unit, g in [x for x in waiting if ready(x[0], x[1], slot)][: MM_CAP if slot < STEPS - 1 else CAP_LAST]:
-                multiply(unit, g)
-                done.add((unit, g))
+            if j >= 2:
+                copy_y(j - 2, both)
+            if slot >= FIRST_MATMUL_SLOT:
+                waiting = [(x, g) for x in range(UNITS) for g in range(PASSES) if (x, g) not in multiplied]
+                for x, g in [pair for pair in waiting if ready(pair[0], pair[1], slot)][:MATMULS_PER_SLOT]:
+                    multiply(x, g)
 
-        def multiply_some(unit, passes):
-            for g in range(passes):
-                if (unit, g) not in done:
-                    multiply(unit, g)
-                    done.add((unit, g))
-
-        assert FIRST_UNIT_SLOT == 12
-        V, S = nc.vector.tensor_copy, nc.scalar.copy
-        turn_et(23)
-        turn_y(10, both, Y_BANKS[0])
-        widen(24)
-        multiply_some(13, 6)
-        multiply_some(14, 2)
-        multiply_some(15, 2)
-        new_momentum(12)
-        quantize_et(22)
-        copy_et(23)
-        turn_et(24)
-        multiply_some(14, 4)
-        multiply_some(15, 4)
-        new_weights(12)
-        store_y(12, both)
-        quantize_et(23)
-        copy_y(10, both)
-        copy_et(24)
-        round_y(11, both, S)
-        new_momentum(13)
-        quantize_et(24)
-        multiply_some(14, 6)
-        multiply_some(15, 6)
-        turn_y(11, both, Y_BANKS[1])
-        new_weights(13)
-        store_y(13, both)
-        quantize_y(9, both)
-        quantize_y(10, both)
-        round_y(12, both, S)
-        turn_y(12, both, acc_bank(12))
-        copy_y(11, both)
-        round_y(13, both, S)
-        turn_y(13, both, acc_bank(13))
-        copy_y(12, both)
-        new_momentum(14)
-        new_momentum(15)
-        new_weights(14)
-        store_y(14, both)
-        new_weights(15)
-        store_y(15, both)
-        round_y(14, both, V)
-        round_y(15, both, V)
-        turn_y(14, both, acc_bank(14))
-        turn_y(15, both, acc_bank(15))
-        copy_y(13, both)
-        copy_y(14, both)
-        copy_y(15, both)
-        for j in range(11, 16):
+        last_step = len(steps) - 1
+        a, b = UNITS - 4, UNITS - 3
+        last_units = range(UNITS - 2, UNITS)
+        turn_et(last_step - 1)
+        turn_y(a - 2, both, RESULT_BANKS[0])
+        widen(last_step)
+        multiply_up_to(range(b + 1), PASSES)
+        multiply_up_to(last_units, 2)
+        new_momentum(a)
+        quantize_et(last_step - 2)
+        copy_et(last_step - 1)
+        turn_et(last_step)
+        multiply_up_to(last_units, 4)
+        new_weights(a)
+        store_y(a, both)
+        quantize_et(last_step - 1)
+        copy_y(a - 2, both)
+        copy_et(last_step)
+        round_y(a - 1, both, on_scalar)
+        new_momentum(b)
+        quantize_et(last_step)
+        multiply_up_to(last_units, PASSES)
+        turn_y(a - 1, both, RESULT_BANKS[1])
+        new_weights(b)
+        store_y(b, both)
+        quantize_y(a - 3, both)
+        quantize_y(a - 2, both)
+        round_y(a, both, on_scalar)
+        turn_y(a, both, acc_bank(a))
+        copy_y(a - 1, both)
+        round_y(b, both, on_vector)
+        turn_y(b, both, acc_bank(b))
+        copy_y(a, both)
+        for j in last_units:
+            new_momentum(j)
+            store_y(j, mom_part)
+        for j in last_units:
+            round_y(j, mom_part, on_scalar)
+        for j in last_units:
+            turn_y(j, mom_part, RESULT_BANKS[j % 2])
+        for j in last_units:
+            new_weights(j)
+            store_y(j, w_part)
+        for j in last_units:
+            round_y(j, w_part, on_vector)
+        for j in last_units:
+            turn_y(j, w_part, acc_bank(j))
+        copy_y(b, both)
+        for parts in (mom_part, w_part):
+            for j in last_units:
+                copy_y(j, parts)
+        for j in range(a - 1, b + 1):
             quantize_y(j, both)
+        for parts in (mom_part, w_part):
+            for j in last_units:
+                quantize_y(j, parts)
         store_scales()

@@ -38,7 +38,8 @@ RING_BANKS = (0, 1, 4, 5)
 
 FIRST_UNIT_SLOT = CHUNKS
 VECTOR_COPY_STEPS = range(10, 18)
-FIRST_MATMUL_SLOT = 6
+VECTOR_WIDENS = (0, 1)
+FIRST_MATMUL_SLOT = 5
 MATMULS_PER_SLOT = 5
 STEP_TO_MATMUL = 3
 CHUNK_TO_MATMUL = 2
@@ -143,12 +144,13 @@ def tile_vision_momentum_sgd_step_b13_kernel(
             for n, g in enumerate(passes):
                 for q in range(PASS // BLOCK):
                     block = g * (PASS // BLOCK) + q
-                    nc.scalar.activation(
-                        out=t[:, n * PASS + q * BLOCK : n * PASS + (q + 1) * BLOCK],
-                        in_=et_bytes[i, g][:, q * BLOCK : (q + 1) * BLOCK].bitcast(FP8),
-                        func=COPY,
-                        scale=et_scale[i][:, block : block + 1],
-                    )
+                    wide = t[:, n * PASS + q * BLOCK : n * PASS + (q + 1) * BLOCK]
+                    codes = et_bytes[i, g][:, q * BLOCK : (q + 1) * BLOCK].bitcast(FP8)
+                    scale = et_scale[i][:, block : block + 1]
+                    if (i, g) == VECTOR_WIDENS:
+                        nc.vector.tensor_scalar(out=wide, in0=codes, scalar1=scale, scalar2=None, op0=MULT)
+                    else:
+                        nc.scalar.activation(out=wide, in_=codes, func=COPY, scale=scale)
             et_wide[s] = t
 
         def turn_et(s):
@@ -302,12 +304,15 @@ def tile_vision_momentum_sgd_step_b13_kernel(
                 )
 
         load_scales(range(0, 1))
-        for n in range(PASSES // 2):
-            load_first_tile(n)
-            load_chunk(n)
-        load_chunk(PASSES // 2)
+        load_first_tile(0)
+        load_first_tile(1)
+        load_chunk(0)
+        load_chunk(1)
+        load_first_tile(2)
+        load_chunk(2)
         load_scales(range(1, 2))
         load_tile(1)
+        load_chunk(3)
         load_pass(2)
         nc.sync.dma_start(out=rate_rows[0:TILES, :], in_=rate.rearrange("(i p) o -> i (p o)", p=P))
         load_scales(range(2, TILES))

from contextlib import ExitStack

import concourse.mybir as mybir
from concourse.masks import make_identity

T, N, K = 3072, 1024, 1024
BLOCK = 32
MU = 0.9
FLOPS = 2 * T * N * K

F32 = mybir.dt.float32
BF16 = mybir.dt.bfloat16
I32 = mybir.dt.int32
U32 = mybir.dt.uint32
U8 = mybir.dt.uint8
FP8 = mybir.dt.float8_e4m3fn
E4M3X4 = mybir.dt.float8_e4m3fn_x4
E5M2X4 = mybir.dt.float8_e5m2_x4
MULT = mybir.AluOpType.mult
ADD = mybir.AluOpType.add
COPY = mybir.ActivationFunctionType.Copy

P = 128
PACK = 4
PASS = P * PACK
PASSES = T // PASS
HALF = 512
HALVES = K // HALF
TILES = N // P
CHUNKS = PASSES * HALVES
UNITS = TILES * HALVES
RESULTS = 2
SLOTS = T * TILES // (2 * PASS)

NUMBERED_BANKS = 6
RESULT_BANKS = (2, 3)
RING_BANKS = (0, 1, 4, 5)

FIRST_UNIT_SLOT = CHUNKS
VECTOR_COPY_STEPS = range(10, 18)
VECTOR_WIDENS = (0, 1)
FIRST_MATMUL_SLOT = 5
MATMULS_PER_SLOT = 5
STEP_TO_MATMUL = 3
CHUNK_TO_MATMUL = 2


def tile_vision_momentum_sgd_step_b13_kernel(
    tc, Et_bytes, Et_scale, A, Mom, W, rate, out_0, out_1, out_2
):
    nc = tc.nc
    on_vector, on_scalar = nc.vector.tensor_copy, nc.scalar.copy
    words_out = out_1.rearrange("g p m t -> g p (m t)").bitcast(I32)
    scales_out = out_2.bitcast(I32)

    with ExitStack() as ctx:
        keep = ctx.enter_context(tc.tile_pool(name="keep", bufs=1))
        flow = ctx.enter_context(tc.tile_pool(name="flow", bufs=3))
        psum = ctx.enter_context(tc.psum_pool(name="psum", bufs=2))
        ctx.enter_context(tc.manual_schedule())

        ident = keep.tile([P, P], F32)
        make_identity(nc, ident[:])
        rate_rows = keep.tile([P, P], BF16)
        nc.gpsimd.memset(rate_rows[:], 0.0)
        ident_bf16 = keep.tile([P, P], BF16)
        make_identity(nc, ident_bf16[:])
        neg_rate = keep.tile([P, TILES], F32)

        def numbered_bank(number, shape, dtype):
            return psum.tile(shape, dtype, name="numbered", tag="bank%d" % number, bufs=1)

        et_scale, et_bytes, a_raw, mom_old, w_old = {}, {}, {}, {}, {}

        def load_scales(tiles):
            blocks = T // BLOCK
            t = keep.tile([P, len(tiles) * blocks], F32, name="et_scale%d" % tiles.start)
            nc.sync.dma_start(
                out=t[:].rearrange("p (i b) -> p i b", b=blocks),
                in_=Et_scale[tiles.start * P : tiles.stop * P, :].rearrange("(i p) b -> p i b", p=P),
            )
            for n, i in enumerate(tiles):
                et_scale[i] = t[:, n * blocks : (n + 1) * blocks]

        def load_et(i, passes, name, bufs):
            t = flow.tile([P, len(passes) * PASS], U8, name=name, bufs=bufs)
            nc.sync.dma_start(out=t[:], in_=Et_bytes[i * P : (i + 1) * P, passes.start * PASS : passes.stop * PASS])
            for n, g in enumerate(passes):
                et_bytes[i, g] = t[:, n * PASS : (n + 1) * PASS]

        def load_first_tile(step):
            load_et(0, range(2 * step, 2 * step + 2), "et_first", 3)

        def load_tile(i):
            load_et(i, range(PASSES), "et_bytes", TILES - 1)

        def load_a(g, halves, name):
            t = flow.tile([P, PACK, len(halves) * HALF], BF16, name=name, bufs=4)
            rows = A[g * PASS : (g + 1) * PASS, halves.start * HALF : halves.stop * HALF]
            nc.sync.dma_start(out=t[:], in_=rows.rearrange("(p t) k -> p t k", t=PACK))
            for n, h in enumerate(halves):
                a_raw[HALVES * g + h] = t[:, :, n * HALF : (n + 1) * HALF]

        def load_chunk(c):
            g, h = divmod(c, HALVES)
            load_a(g, range(h, h + 1), "a_first")

        def load_pass(g):
            load_a(g, range(HALVES), "a_raw")

        state_tiles = 4

        def load_state(i):
            for src, dst, name in ((Mom, mom_old, "mom_old"), (W, w_old, "w_old")):
                t = flow.tile([P, K], BF16, name=name, bufs=state_tiles)
                nc.sync.dma_start(out=t[:], in_=src[i * P : (i + 1) * P, :])
                dst[i] = t

        a_grouped, a_codes, a_scales = {}, {}, {}

        def interleave_a(c):
            t = flow.tile([P, HALF * PACK], BF16, name="a_grouped", align_bytes=64)
            nc.vector.tensor_copy(
                out=t[:].rearrange("p (c i t) -> p c t i", i=4, t=PACK),
                in_=a_raw[c].rearrange("p t (c i) -> p c t i", i=4),
            )
            a_grouped[c] = t

        def quantize_a(c):
            codes = keep.tile([P, HALF], U32, name="a_codes%d" % c, align_bytes=64)
            scales = keep.tile([P, HALF], U8, name="a_scales%d" % c, align_bytes=64)
            nc.vector.quantize_mx(out=codes[:].bitcast(E4M3X4), scales=scales[:], in_=a_grouped[c][:])
            a_codes[c] = codes
            a_scales[c] = scales

        steps = [(i, range(g, g + 2)) for i in range(TILES) for g in range(0, PASSES, 2)]
        steps = steps[:-1] + [(TILES - 1, range(g, g + 1)) for g in (PASSES - 2, PASSES - 1)]
        step_of = {(i, g): s for s, (i, passes) in enumerate(steps) for g in passes}
        et_wide, et_bank, et_grouped, et_codes, et_scales = {}, {}, {}, {}, {}

        def widen(s):
            i, passes = steps[s]
            t = flow.tile([P, len(passes) * PASS], BF16, name="et_wide")
            for n, g in enumerate(passes):
                for q in range(PASS // BLOCK):
                    block = g * (PASS // BLOCK) + q
                    wide = t[:, n * PASS + q * BLOCK : n * PASS + (q + 1) * BLOCK]
                    codes = et_bytes[i, g][:, q * BLOCK : (q + 1) * BLOCK].bitcast(FP8)
                    scale = et_scale[i][:, block : block + 1]
                    if (i, g) == VECTOR_WIDENS:
                        nc.vector.tensor_scalar(out=wide, in0=codes, scalar1=scale, scalar2=None, op0=MULT)
                    else:
                        nc.scalar.activation(out=wide, in_=codes, func=COPY, scale=scale)
            et_wide[s] = t

        def turn_et(s):
            count = len(steps[s][1])
            bank = psum.tile([P, count * 2 * P], F32, name="et_bank")
            pairs = et_wide[s][:].bitcast(F32)
            for n in range(count):
                for u in range(2):
                    nc.tensor.transpose(
                        bank[:, (2 * n + u) * P : (2 * n + u + 1) * P],
                        pairs[:, 2 * P * n + u : 2 * P * (n + 1) : 2],
                        ident[:],
                    )
            et_bank[s] = bank

        def copy_bank(engine_copy, bank, name):
            t = flow.tile([P, 2 * bank.shape[1]], BF16, name=name, bufs=8, align_bytes=64)
            engine_copy(
                out=t[:].bitcast(F32).rearrange("p (n r u) -> p n r u", r=P, u=2),
                in_=bank[:].rearrange("p (n u r) -> p n r u", r=P, u=2),
            )
            return t

        def copy_et(s):
            et_grouped[s] = copy_bank(on_vector if s in VECTOR_COPY_STEPS else on_scalar, et_bank[s], "et_grouped")

        def quantize_et(s):
            i, passes = steps[s]
            codes = flow.tile([P, len(passes) * P], U32, name="et_codes", bufs=10, align_bytes=64)
            scales = flow.tile([P, len(passes) * P], U8, name="et_scales", bufs=10, align_bytes=64)
            nc.vector.quantize_mx(out=codes[:].bitcast(E5M2X4), scales=scales[:], in_=et_grouped[s][:])
            for n, g in enumerate(passes):
                et_codes[i, g] = codes[:, n * P : (n + 1) * P]
                et_scales[i, g] = scales[:, n * P : (n + 1) * P]

        acc = {}
        multiplied = set()

        def acc_bank(j):
            return j if j < NUMBERED_BANKS else RING_BANKS[(j - NUMBERED_BANKS) % len(RING_BANKS)]

        def multiply(j, g):
            i, h = divmod(j, HALVES)
            if g == 0:
                acc[j] = numbered_bank(acc_bank(j), [P, HALF], F32)
            c = HALVES * g + h
            nc.tensor.matmul_mx(
                out=acc[j][:],
                lhsT=et_codes[i, g].bitcast(E5M2X4),
                lhsT_scale=et_scales[i, g],
                rhs=a_codes[c][:].bitcast(E4M3X4),
                rhs_scale=a_scales[c][:],
                start=(g == 0),
                stop=(g == PASSES - 1),
            )
            multiplied.add((j, g))

        def multiply_up_to(units, passes):
            for j in units:
                for g in range(passes):
                    if (j, g) not in multiplied:
                        multiply(j, g)

        both, mom_part, w_part = range(RESULTS), range(0, 1), range(1, 2)
        y, y_sorted, y_bank, y_grouped, y_codes = {}, {}, {}, {}, {}
        y_scales = keep.tile([P, HALVES * RESULTS * N], U8, align_bytes=64)

        def new_momentum(j):
            i, h = divmod(j, HALVES)
            assert (j, PASSES - 1) in multiplied
            t = flow.tile([P, RESULTS * HALF], F32, name="y", bufs=5)
            nc.vector.scalar_tensor_tensor(
                out=t[:, 0:HALF],
                in0=mom_old[i][:, h * HALF : (h + 1) * HALF],
                scalar=MU,
                in1=acc[j][:],
                op0=MULT,
                op1=ADD,
            )
            y[j] = t

        def new_weights(j):
            i, h = divmod(j, HALVES)
            nc.vector.scalar_tensor_tensor(
                out=y[j][:, HALF : 2 * HALF],
                in0=y[j][:, 0:HALF],
                scalar=neg_rate[:, i : i + 1],
                in1=w_old[i][:, h * HALF : (h + 1) * HALF],
                op0=MULT,
                op1=ADD,
            )

        def store_y(j, parts):
            i, h = divmod(j, HALVES)
            rows = out_0[parts.start : parts.stop, i * P : (i + 1) * P, h * HALF : (h + 1) * HALF]
            nc.sync.dma_start(
                out=rows.rearrange("s p k -> p s k"),
                in_=y[j][:, parts.start * HALF : parts.stop * HALF].rearrange("p (s k) -> p s k", k=HALF),
            )

        def round_y(j, parts, engine_copy):
            t = flow.tile([P, len(parts) * HALF], BF16, name="y_sorted", bufs=4)
            engine_copy(
                out=t[:].rearrange("p (n u q e) -> p n u q e", u=2, q=P, e=2),
                in_=y[j][:, parts.start * HALF : parts.stop * HALF].rearrange(
                    "p (n q u e) -> p n u q e", u=2, q=P, e=2
                ),
            )
            y_sorted[j, parts] = t

        def turn_y(j, parts, bank_number):
            bank = numbered_bank(bank_number, [P, len(parts) * 2 * P], F32)
            pairs = y_sorted[j, parts][:].bitcast(F32)
            for run in range(len(parts) * 2):
                nc.tensor.transpose(bank[:, run * P : (run + 1) * P], pairs[:, run * P : (run + 1) * P], ident[:])
            y_bank[j, parts] = bank

        def copy_y(j, parts):
            y_grouped[j, parts] = copy_bank(on_scalar, y_bank[j, parts], "y_grouped")

        code_groups = [range(i, i + 2) for i in range(0, TILES - 2, 2)]
        code_groups = code_groups + [range(i, i + 1) for i in (TILES - 2, TILES - 1)]

        def quantize_y(j, parts):
            i, h = divmod(j, HALVES)
            group = [tiles for tiles in code_groups if i in tiles][0]
            width = len(group) * P
            if (group, h) not in y_codes:
                y_codes[group, h] = flow.tile([P, RESULTS * width], U32, name="y_codes", bufs=6, align_bytes=64)
            codes = y_codes[group, h]
            for n, s in enumerate(parts):
                first_code = s * width + (i - group.start) * P
                first_scale = (RESULTS * h + s) * N + i * P
                nc.vector.quantize_mx(
                    out=codes[:, first_code : first_code + P].bitcast(E4M3X4),
                    scales=y_scales[:, first_scale : first_scale + P],
                    in_=y_grouped[j, parts][:, n * PASS : (n + 1) * PASS],
                )
            if i == group.stop - 1 and parts.stop == RESULTS:
                columns = words_out[h].rearrange("p (s n) -> p s n", s=RESULTS)
                nc.sync.dma_start(
                    out=columns[:, :, group.start * P : group.stop * P],
                    in_=codes[:].bitcast(I32).rearrange("p (s n) -> p s n", s=RESULTS),
                )

        def store_scales():
            for q in range(P // 32):
                (nc.scalar, nc.sync)[q % 2].dma_start(
                    out=scales_out[:, 4 * q : 4 * q + 4, :].rearrange("h r m -> r h m"),
                    in_=y_scales[32 * q : 32 * q + 4, :].bitcast(I32).rearrange("r (h m) -> r h m", h=HALVES),
                )

        load_scales(range(0, 1))
        load_first_tile(0)
        load_first_tile(1)
        load_chunk(0)
        load_chunk(1)
        load_first_tile(2)
        load_chunk(2)
        load_scales(range(1, 2))
        load_tile(1)
        load_chunk(3)
        load_pass(2)
        nc.sync.dma_start(out=rate_rows[0:TILES, :], in_=rate.rearrange("(i p) o -> i (p o)", p=P))
        load_scales(range(2, TILES))
        load_pass(3)
        load_tile(2)
        load_pass(4)
        load_tile(3)
        load_pass(5)
        for i in range(state_tiles):
            load_state(i)
            load_tile(TILES - state_tiles + i)

        chunk_slot = [max(c - 1, 0) for c in range(CHUNKS)]

        def ready(j, g, slot):
            i, h = divmod(j, HALVES)
            earlier = [x for x in range(j) if acc_bank(x) == acc_bank(j)]
            bank_free = not earlier or FIRST_UNIT_SLOT + earlier[-1] <= slot
            step_done = step_of[i, g] + STEP_TO_MATMUL <= slot
            chunk_done = chunk_slot[HALVES * g + h] + CHUNK_TO_MATMUL <= slot
            return bank_free and step_done and chunk_done

        rate_bank = numbered_bank(NUMBERED_BANKS - 1, [P, P], BF16)
        interleaved = []
        for slot in range(SLOTS):
            j = slot - FIRST_UNIT_SLOT
            if j >= HALVES and j % HALVES == 0 and j // HALVES - 1 + state_tiles < TILES:
                load_state(j // HALVES - 1 + state_tiles)
            if slot == FIRST_MATMUL_SLOT:
                nc.tensor.transpose(rate_bank[:], rate_rows[:], ident_bf16[:])
            if slot == FIRST_MATMUL_SLOT + 1:
                nc.scalar.activation(out=neg_rate[:], in_=rate_bank[:, 0:TILES], func=COPY, scale=-1.0)
            if slot >= 1:
                turn_et(slot - 1)
            if j >= 0:
                new_momentum(j)
            if j >= 1:
                round_y(j - 1, both, on_vector)
            if j >= 2:
                turn_y(j - 2, both, RESULT_BANKS[j % 2])
            widen(slot)
            chunks = [c for c in range(CHUNKS) if chunk_slot[c] == slot]
            for c in chunks:
                interleave_a(c)
                if interleaved:
                    quantize_a(interleaved.pop())
                interleaved.append(c)
            if interleaved and not chunks:
                quantize_a(interleaved.pop())
            if j >= 3:
                quantize_y(j - 3, both)
            if j >= 0:
                new_weights(j)
                store_y(j, both)
            if slot >= 2:
                quantize_et(slot - 2)
            if slot >= 1:
                copy_et(slot - 1)
            if j >= 2:
                copy_y(j - 2, both)
            if slot >= FIRST_MATMUL_SLOT:
                waiting = [(x, g) for x in range(UNITS) for g in range(PASSES) if (x, g) not in multiplied]
                for x, g in [pair for pair in waiting if ready(pair[0], pair[1], slot)][:MATMULS_PER_SLOT]:
                    multiply(x, g)

        last_step = len(steps) - 1
        a, b = UNITS - 4, UNITS - 3
        last_units = range(UNITS - 2, UNITS)
        turn_et(last_step - 1)
        turn_y(a - 2, both, RESULT_BANKS[0])
        widen(last_step)
        multiply_up_to(range(b + 1), PASSES)
        multiply_up_to(last_units, 2)
        new_momentum(a)
        quantize_et(last_step - 2)
        copy_et(last_step - 1)
        turn_et(last_step)
        multiply_up_to(last_units, 4)
        new_weights(a)
        store_y(a, both)
        quantize_et(last_step - 1)
        copy_y(a - 2, both)
        copy_et(last_step)
        round_y(a - 1, both, on_scalar)
        new_momentum(b)
        quantize_et(last_step)
        multiply_up_to(last_units, PASSES)
        turn_y(a - 1, both, RESULT_BANKS[1])
        new_weights(b)
        store_y(b, both)
        quantize_y(a - 3, both)
        quantize_y(a - 2, both)
        round_y(a, both, on_scalar)
        turn_y(a, both, acc_bank(a))
        copy_y(a - 1, both)
        round_y(b, both, on_vector)
        turn_y(b, both, acc_bank(b))
        copy_y(a, both)
        for j in last_units:
            new_momentum(j)
            store_y(j, mom_part)
        for j in last_units:
            round_y(j, mom_part, on_scalar)
        for j in last_units:
            turn_y(j, mom_part, RESULT_BANKS[j % 2])
        for j in last_units:
            new_weights(j)
            store_y(j, w_part)
        for j in last_units:
            round_y(j, w_part, on_vector)
        for j in last_units:
            turn_y(j, w_part, acc_bank(j))
        copy_y(b, both)
        for parts in (mom_part, w_part):
            for j in last_units:
                copy_y(j, parts)
        for j in range(a - 1, b + 1):
            quantize_y(j, both)
        for parts in (mom_part, w_part):
            for j in last_units:
                quantize_y(j, parts)
        store_scales()
